import numpy as np
import ml_dtypes


def mxq(x, axis, fmt="e4m3"):
    dtype, down = {"e4m3": (ml_dtypes.float8_e4m3fn, 7), "e5m2": (ml_dtypes.float8_e5m2, 14)}[fmt]
    v = np.moveaxis(np.asarray(x, np.float32).astype(ml_dtypes.bfloat16).astype(np.float64), axis, -1)
    blocks = v.reshape(v.shape[:-1] + (-1, 32))
    amax = np.abs(blocks).max(-1, keepdims=True)
    byte = np.maximum(np.where(amax > 0, np.frexp(amax)[1] - 1 + 127, 0) - down, 1)
    scale = np.exp2(byte - 127.0)
    codes = (blocks / scale).astype(np.float32).astype(dtype).astype(np.float64)
    return np.moveaxis((codes * scale).reshape(v.shape), -1, axis)


WIDE = False


def mx_kscale(k):
    if not WIDE:
        return np.ones(k)
    levels = np.array([10, -10, 5, -5, 0])
    if k % 512:
        return np.exp2(np.random.permutation(np.resize(levels, k // 32))).repeat(32)
    a = np.empty((k // 512, 16))
    for p in range(k // 512):
        a[p, :8] = np.random.permutation(np.resize(levels, 8))
        for g in range(8):
            far = levels[np.abs(levels - a[p, g]) >= 10]
            a[p, g + 8] = far[np.random.randint(len(far))]
    return np.exp2(a.ravel()).repeat(32)


def f64(x):
    return np.asarray(x).astype(np.float64)


def striped(idx):
    return np.tile(idx.reshape(-1, 16).T, (8, 1)).astype(np.uint16)


def unstriped(offs):
    return offs[:16].T.reshape(-1).astype(np.int64)


E2M1 = np.array([0.0, 0.5, 1.0, 1.5, 2.0, 3.0, 4.0, 6.0, -0.0, -0.5, -1.0, -1.5, -2.0, -3.0, -4.0, -6.0])


def pack_weight(w, fmt):
    k, n = w.shape
    w = f64(np.asarray(w, np.float32).astype(ml_dtypes.bfloat16)).reshape(k // 32, 32, n)
    amax = np.abs(w).max(1)
    if fmt == "e4m3":
        byte = np.frexp(amax)[1] - 1 + 127 - 7
    else:
        mant, ex = np.frexp(amax / 6.0)
        byte = np.where(mant > 0.5, ex, ex - 1) + 127
    byte = np.clip(np.where(amax > 0, byte, 1), 1, 254)
    scaled = (w * np.exp2(127.0 - byte)[:, None, :]).reshape(k, n).astype(np.float32)
    by_word = np.ascontiguousarray(scaled.reshape(k // 512, 128, 4, n).transpose(0, 1, 3, 2))
    if fmt == "e4m3":
        words = by_word.astype(ml_dtypes.float8_e4m3fn).view(np.uint8)
    else:
        c = by_word.astype(ml_dtypes.float4_e2m1fn).view(np.uint8) & 0xF
        words = (c[..., 0::2] | (c[..., 1::2] << 4)).reshape(k // 512, 128, 2 * n)
    return np.ascontiguousarray(words), np.ascontiguousarray(byte.astype(np.uint8).reshape(k // 512, 16, n))


def unpack_weight(words, scales, fmt):
    g, _, n = scales.shape
    words = np.ascontiguousarray(words).reshape(g, 128, n, -1)
    if fmt == "e4m3":
        vals = words.view(ml_dtypes.float8_e4m3fn).astype(np.float64)
    else:
        nib = np.empty((g, 128, n, 4), np.uint8)
        nib[..., 0::2] = words & 0xF
        nib[..., 1::2] = words >> 4
        vals = E2M1[nib]
    vals = vals * np.repeat(np.exp2(scales.astype(np.float64) - 127.0), 8, axis=1)[..., None]
    return vals.transpose(0, 1, 3, 2).reshape(g * 512, n)


def silu(v):
    return v / (1.0 + np.exp(-np.maximum(v, -700.0)))


K, T, E, C, H, N = 1024, 1024, 4, 256, 512, 128


def by_expert(wq, xq):
    return np.concatenate([wq[e].T @ xq[:, e * C:(e + 1) * C] for e in range(E)], axis=1)


def setup_inputs():
    n = np.random.standard_normal
    s = mx_kscale(K)[:, None]
    u = mx_kscale(H)
    x = pack_weight(n((K, T)) * s, "e4m3")
    return {
        "x_words": x[0],
        "x_scales": x[1],
        "w1": (n((E, K, H)) / np.sqrt(K) / s[None] * u[None, None, :]).astype(np.float32),
        "w2": (n((E, H, N)) / np.sqrt(H) / u[None, :, None]).astype(np.float32),
        "gate": np.tile(np.random.uniform(0.2, 1.0, E * C), (N, 1)).astype(np.float32),
        "offs": striped(np.random.permutation(T)[:E * C]),
        "dst": striped(np.random.permutation(T)[:E * C]),
    }


def reference(x_words, x_scales, w1, w2, gate, offs, dst):
    idx = unstriped(offs)
    xq = unpack_weight(x_words, x_scales, "e4m3")[:, idx]
    h = silu(by_expert(mxq(f64(w1), 1, "e4m3"), xq))
    y = by_expert(mxq(f64(w2), 1, "e4m3"), mxq(h, 0, "e4m3"))
    out = np.zeros((N, T))
    out[:, unstriped(dst)] = f64(gate) * y
    return out

@@ -1,0 +1,302 @@
+from contextlib import ExitStack
+
+import concourse.mybir as mybir
+
+K, T, E, C, H, N = 1024, 1024, 4, 256, 512, 128
+FLOPS = 2 * E * C * (K * H + H * N)
+
+F32 = mybir.dt.float32
+BF16 = mybir.dt.bfloat16
+I32 = mybir.dt.int32
+U32 = mybir.dt.uint32
+U16 = mybir.dt.uint16
+U8 = mybir.dt.uint8
+FP8X4 = mybir.dt.float8_e4m3fn_x4
+SILU = mybir.ActivationFunctionType.Silu
+MULT = mybir.AluOpType.mult
+
+P = 128
+PACK = 4
+K_PASS = P * PACK
+PASSES = K // K_PASS
+HALF = C // 2
+LIST_COLS = C // 16
+
+VECTOR_SHARE = [[0,0],[24,32],[32,32],[32,64]]
+W2_ON_SCALAR = [1,0,0,1]
+
+
+def tile_moe_two_mlp_silu_kernel(
+    tc, x_words, x_scales, w1, w2, gate, offs, dst, out
+):
+    nc = tc.nc
+    with ExitStack() as ctx:
+        keep = ctx.enter_context(tc.tile_pool(name="keep", bufs=1))
+        psum_a = ctx.enter_context(tc.psum_pool(name="psum_a", bufs=4))
+        psum_y = ctx.enter_context(tc.psum_pool(name="psum_y", bufs=2))
+
+        def sb(name, shape, dtype):
+            return keep.tile(shape, dtype, name=name, align_bytes=64)
+
+        offs_sb = keep.tile([P, E * LIST_COLS], U16, name="offs_sb")
+        dst_sb = keep.tile([P, E * LIST_COLS], U16, name="dst_sb")
+        tok_scales = sb("tok_scales", [P, T // 4], I32)
+        tok_words = [sb("tok_words%d" % o, [P, T], I32) for o in range(PASSES)]
+        w1_raw = [[sb("w1_raw%d_%d" % (e, o), [P, PACK, H], F32) for o in range(PASSES)] for e in range(E)]
+        w1_bf = [[sb("w1_bf%d_%d" % (e, o), [P, PACK, P, PACK], BF16) for o in range(PASSES)] for e in range(E)]
+        w1_codes = [[sb("w1_codes%d_%d" % (e, o), [P, H], U32) for o in range(PASSES)] for e in range(E)]
+        w1_scales = [[sb("w1_scales%d_%d" % (e, o), [P, H], U8) for o in range(PASSES)] for e in range(E)]
+        w2_raw = [sb("w2_raw%d" % e, [P, PACK, N], F32) for e in range(E)]
+        w2_bf = [sb("w2_bf%d" % e, [P, N, PACK], BF16) for e in range(E)]
+        w2_codes = [sb("w2_codes%d" % e, [P, N], U32) for e in range(E)]
+        w2_scales = [sb("w2_scales%d" % e, [P, N], U8) for e in range(E)]
+        gate_sb = [sb("gate_sb%d" % e, [P, C], F32) for e in range(E)]
+        slot_words = [[sb("slot_words%d_%d" % (e, o), [P, C], U32) for o in range(PASSES)] for e in range(E)]
+        slot_scales = [sb("slot_scales%d" % e, [P, C], U8) for e in range(E)]
+        h_bf = [sb("h_bf%d" % e, [P, C, PACK], BF16) for e in range(E)]
+        h_codes = [sb("h_codes%d" % e, [P, C], U32) for e in range(E)]
+        h_scales = [sb("h_scales%d" % e, [P, C], U8) for e in range(E)]
+        y_sb = [sb("y_sb%d" % e, [P, C], F32) for e in range(E)]
+        out_sb = sb("out_sb", [P, T], F32)
+        warm_in = sb("warm_in", [P, 16], F32)
+        warm_out = sb("warm_out", [P, 16], F32)
+
+        def load_w1(e, o):
+            rows = w1[e, o * K_PASS : (o + 1) * K_PASS, :]
+            nc.sync.dma_start(out=w1_raw[e][o][:], in_=rows.rearrange("(p j) c -> p j c", j=PACK))
+
+        def load_words(o):
+            nc.sync.dma_start(out=tok_words[o][:], in_=x_words[o].rearrange("p t r -> p (t r)").bitcast(I32))
+
+        def load_w2(e):
+            nc.sync.dma_start(out=w2_raw[e][:], in_=w2[e].rearrange("(p j) n -> p j n", j=PACK))
+
+        def load_gate(e):
+            nc.sync.dma_start(out=gate_sb[e][:], in_=gate[:, e * C : (e + 1) * C])
+
+        def gather_scales(e):
+            window = tok_scales[:].bitcast(U8)
+            nc.vector.tensor_copy(slot_scales[e][:], window.indirect(offs_sb[:, e * LIST_COLS : (e + 1) * LIST_COLS]))
+
+        def gather_words(e, o):
+            window = tok_words[o][:].bitcast(U32)
+            nc.vector.tensor_copy(slot_words[e][o][:], window.indirect(offs_sb[:, e * LIST_COLS : (e + 1) * LIST_COLS]))
+
+        def cast_w1_part(copy, e, o, m0, m1):
+            copy(
+                w1_bf[e][o][:, :, m0:m1, :].rearrange("p t m j -> p m j t"),
+                w1_raw[e][o][:, :, PACK * m0 : PACK * m1].rearrange("p j (m t) -> p m j t", t=PACK),
+            )
+
+        def cast_w1_scalar(e, o):
+            cast_w1_part(nc.scalar.copy, e, o, VECTOR_SHARE[e][o], P)
+
+        def cast_w1_vector(e, o):
+            if VECTOR_SHARE[e][o]:
+                cast_w1_part(nc.vector.tensor_copy, e, o, 0, VECTOR_SHARE[e][o])
+
+        def quantise_w1(e, o, t0, t1):
+            nc.vector.quantize_mx(
+                out=w1_codes[e][o][:, t0 * P : t1 * P].bitcast(FP8X4),
+                scales=w1_scales[e][o][:, t0 * P : t1 * P],
+                in_=w1_bf[e][o][:, t0:t1, :, :].rearrange("p t m j -> p (t m j)"),
+            )
+
+        def cast_w2(e):
+            copy = nc.scalar.copy if W2_ON_SCALAR[e] else nc.vector.tensor_copy
+            copy(
+                w2_bf[e][:].rearrange("p (c i) j -> p c j i", i=4),
+                w2_raw[e][:].rearrange("p j (c i) -> p c j i", i=4),
+            )
+
+        def quantise_w2(e):
+            nc.vector.quantize_mx(
+                out=w2_codes[e][:].bitcast(FP8X4),
+                scales=w2_scales[e][:],
+                in_=w2_bf[e][:].rearrange("p n j -> p (n j)"),
+            )
+
+        banks = {}
+
+        def first_layer(e, o, half, ts):
+            cols = slice(half * HALF, (half + 1) * HALF)
+            if (e, half) not in banks:
+                banks[(e, half)] = psum_a.tile([P, PACK, HALF], F32, name="bank")
+            for t in ts:
+                nc.tensor.matmul_mx(
+                    out=banks[(e, half)][:, t, :],
+                    lhsT=w1_codes[e][o][:, t * P : (t + 1) * P].bitcast(FP8X4),
+                    lhsT_scale=w1_scales[e][o][:, t * P : (t + 1) * P],
+                    rhs=slot_words[e][o][:, cols].bitcast(FP8X4),
+                    rhs_scale=slot_scales[e][4 * o : P, cols],
+                    start=(o == 0 and t == 0),
+                    stop=(o == PASSES - 1 and t == PACK - 1),
+                )
+
+        def silu(e, half):
+            cols = slice(half * HALF, (half + 1) * HALF)
+            nc.scalar.activation(h_bf[e][:, cols, :], banks[(e, half)][:].rearrange("p t n -> p n t"), SILU)
+
+        def quantise_h(e, c0, c1):
+            nc.vector.quantize_mx(
+                out=h_codes[e][:, c0:c1].bitcast(FP8X4),
+                scales=h_scales[e][:, c0:c1],
+                in_=h_bf[e][:, c0:c1, :].rearrange("p n t -> p (n t)"),
+            )
+
+        y_banks = {}
+
+        def second_layer(e, c0, c1):
+            y_banks[(e, c0)] = psum_y.tile([P, c1 - c0], F32, name="y_ps")
+            nc.tensor.matmul_mx(
+                out=y_banks[(e, c0)][:],
+                lhsT=w2_codes[e][:].bitcast(FP8X4),
+                lhsT_scale=w2_scales[e][:],
+                rhs=h_codes[e][:, c0:c1].bitcast(FP8X4),
+                rhs_scale=h_scales[e][:, c0:c1],
+                start=True,
+                stop=True,
+            )
+
+        def copy_y(e, c0, c1):
+            nc.scalar.copy(y_sb[e][:, c0:c1], y_banks[(e, c0)][:])
+
+        def scatter(e, c0, c1):
+            places = dst_sb[:, (e * C + c0) // 16 : (e * C + c1) // 16]
+            nc.vector.tensor_tensor(out_sb[:].indirect(places), y_sb[e][:, c0:c1], gate_sb[e][:, c0:c1], MULT)
+
+        def load_scales():
+            for q in range(4):
+                nc.sync.dma_start(
+                    out=tok_scales[32 * q : 32 * q + 4 * PASSES, :],
+                    in_=x_scales[:, 4 * q : 4 * q + 4, :].bitcast(I32),
+                )
+
+        nc.vector.memset(tok_scales[:], 0)
+        nc.gpsimd.memset(warm_in[:], 0.0)
+        nc.scalar.activation(warm_out[:], warm_in[:], SILU)
+        nc.sync.dma_start(offs_sb[:], offs)
+        load_words(0)
+        load_scales()
+        load_w1(0, 0)
+        load_words(1)
+        load_w1(0, 1)
+        load_w2(0)
+        load_w1(1, 0)
+        load_w1(1, 1)
+        nc.sync.dma_start(dst_sb[:], dst)
+        load_gate(0)
+        load_w2(1)
+        load_w1(2, 0)
+        load_w1(2, 1)
+        load_gate(1)
+        load_w2(2)
+        load_w1(3, 0)
+        load_w1(3, 1)
+        load_gate(2)
+        load_w2(3)
+        load_gate(3)
+        gather_words(0, 0)
+        gather_words(1, 0)
+        gather_words(2, 0)
+        gather_words(3, 0)
+        gather_scales(0)
+        gather_scales(1)
+        cast_w1_scalar(0, 0)
+        cast_w1_vector(0, 0)
+        gather_words(0, 1)
+        gather_words(1, 1)
+        quantise_w1(0, 0, 0, 4)
+        first_layer(0, 0, 0, range(4))
+        first_layer(0, 0, 1, range(4))
+        gather_scales(2)
+        gather_scales(3)
+        gather_words(2, 1)
+        cast_w1_scalar(0, 1)
+        cast_w1_vector(0, 1)
+        quantise_w1(0, 1, 0, 2)
+        first_layer(0, 1, 0, (0, 1))
+        first_layer(0, 1, 1, (0, 1))
+        quantise_w1(0, 1, 2, 4)
+        first_layer(0, 1, 0, (2, 3))
+        first_layer(0, 1, 1, (2, 3))
+        gather_words(3, 1)
+        cast_w1_vector(1, 0)
+        cast_w1_scalar(1, 0)
+        silu(0, 0)
+        silu(0, 1)
+        cast_w1_scalar(1, 1)
+        quantise_w1(1, 0, 0, 4)
+        cast_w1_vector(1, 1)
+        cast_w2(0)
+        first_layer(1, 0, 0, range(4))
+        first_layer(1, 0, 1, range(4))
+        quantise_h(0, 0, 256)
+        quantise_w2(0)
+        quantise_w1(1, 1, 0, 2)
+        second_layer(0, 0, 256)
+        quantise_w1(1, 1, 2, 4)
+        copy_y(0, 0, 256)
+        first_layer(1, 1, 0, (0, 1))
+        first_layer(1, 1, 1, (0, 1))
+        first_layer(1, 1, 0, (2, 3))
+        scatter(0, 0, 128)
+        first_layer(1, 1, 1, (2, 3))
+        cast_w1_vector(2, 0)
+        cast_w1_scalar(2, 0)
+        silu(1, 0)
+        scatter(0, 128, 256)
+        silu(1, 1)
+        cast_w1_scalar(2, 1)
+        quantise_w1(2, 0, 0, 4)
+        cast_w1_vector(2, 1)
+        cast_w2(1)
+        first_layer(2, 0, 0, range(4))
+        first_layer(2, 0, 1, range(4))
+        quantise_h(1, 0, 256)
+        quantise_w2(1)
+        quantise_w1(2, 1, 0, 2)
+        second_layer(1, 0, 256)
+        quantise_w1(2, 1, 2, 4)
+        copy_y(1, 0, 256)
+        first_layer(2, 1, 0, (0, 1))
+        first_layer(2, 1, 1, (0, 1))
+        first_layer(2, 1, 0, (2, 3))
+        scatter(1, 0, 128)
+        first_layer(2, 1, 1, (2, 3))
+        cast_w1_vector(3, 0)
+        cast_w1_scalar(3, 0)
+        silu(2, 0)
+        scatter(1, 128, 256)
+        silu(2, 1)
+        cast_w1_scalar(3, 1)
+        quantise_w1(3, 0, 0, 4)
+        cast_w1_vector(3, 1)
+        cast_w2(2)
+        first_layer(3, 0, 0, range(4))
+        first_layer(3, 0, 1, range(4))
+        quantise_h(2, 0, 256)
+        quantise_w2(2)
+        quantise_w1(3, 1, 0, 2)
+        second_layer(2, 0, 256)
+        quantise_w1(3, 1, 2, 4)
+        copy_y(2, 0, 256)
+        first_layer(3, 1, 0, (0, 1))
+        first_layer(3, 1, 1, (0, 1))
+        first_layer(3, 1, 0, (2, 3))
+        scatter(2, 0, 128)
+        first_layer(3, 1, 1, (2, 3))
+        cast_w2(3)
+        scatter(2, 128, 256)
+        silu(3, 0)
+        silu(3, 1)
+        quantise_w2(3)
+        quantise_h(3, 0, 128)
+        second_layer(3, 0, 128)
+        copy_y(3, 0, 128)
+        quantise_h(3, 128, 256)
+        second_layer(3, 128, 256)
+        scatter(3, 0, 128)
+        copy_y(3, 128, 256)
+        scatter(3, 128, 256)
+        nc.sync.dma_start(out=out, in_=out_sb[:])

@@ -22,8 +22,8 @@ PASSES = K // K_PASS
 HALF = C // 2
 LIST_COLS = C // 16
 
-VECTOR_SHARE = [[0,0],[24,32],[32,32],[32,64]]
-W2_ON_SCALAR = [1,0,0,1]
+VECTOR_SHARE = [[0,24],[48,80],[64,24],[48,96]]
+W2_ON_SCALAR = [0,1,1,1]
 
 
 def tile_moe_two_mlp_silu_kernel(
@@ -32,7 +32,7 @@ def tile_moe_two_mlp_silu_kernel(
     nc = tc.nc
     with ExitStack() as ctx:
         keep = ctx.enter_context(tc.tile_pool(name="keep", bufs=1))
-        psum_a = ctx.enter_context(tc.psum_pool(name="psum_a", bufs=4))
+        psum_a = ctx.enter_context(tc.psum_pool(name="psum_a", bufs=6))
         psum_y = ctx.enter_context(tc.psum_pool(name="psum_y", bufs=2))
 
         def sb(name, shape, dtype):
@@ -51,8 +51,8 @@ def tile_moe_two_mlp_silu_kernel(
         w2_codes = [sb("w2_codes%d" % e, [P, N], U32) for e in range(E)]
         w2_scales = [sb("w2_scales%d" % e, [P, N], U8) for e in range(E)]
         gate_sb = [sb("gate_sb%d" % e, [P, C], F32) for e in range(E)]
-        slot_words = [[sb("slot_words%d_%d" % (e, o), [P, C], U32) for o in range(PASSES)] for e in range(E)]
-        slot_scales = [sb("slot_scales%d" % e, [P, C], U8) for e in range(E)]
+        slot_words = [[sb("slot_words%d_%d" % (g, o), [P, 2 * C], U32) for o in range(PASSES)] for g in range(E // 2)]
+        slot_scales = [sb("slot_scales%d" % g, [P, 2 * C], U8) for g in range(E // 2)]
         h_bf = [sb("h_bf%d" % e, [P, C, PACK], BF16) for e in range(E)]
         h_codes = [sb("h_codes%d" % e, [P, C], U32) for e in range(E)]
         h_scales = [sb("h_scales%d" % e, [P, C], U8) for e in range(E)]
@@ -76,11 +76,11 @@ def tile_moe_two_mlp_silu_kernel(
 
         def gather_scales(e):
             window = tok_scales[:].bitcast(U8)
-            nc.vector.tensor_copy(slot_scales[e][:], window.indirect(offs_sb[:, e * LIST_COLS : (e + 1) * LIST_COLS]))
+            nc.vector.tensor_copy(slot_scales[e // 2][:], window.indirect(offs_sb[:, e * LIST_COLS : (e + 2) * LIST_COLS]))
 
         def gather_words(e, o):
             window = tok_words[o][:].bitcast(U32)
-            nc.vector.tensor_copy(slot_words[e][o][:], window.indirect(offs_sb[:, e * LIST_COLS : (e + 1) * LIST_COLS]))
+            nc.vector.tensor_copy(slot_words[e // 2][o][:], window.indirect(offs_sb[:, e * LIST_COLS : (e + 2) * LIST_COLS]))
 
         def cast_w1_part(copy, e, o, m0, m1):
             copy(
@@ -119,7 +119,7 @@ def tile_moe_two_mlp_silu_kernel(
         banks = {}
 
         def first_layer(e, o, half, ts):
-            cols = slice(half * HALF, (half + 1) * HALF)
+            cols = slice((e % 2) * C + half * HALF, (e % 2) * C + (half + 1) * HALF)
             if (e, half) not in banks:
                 banks[(e, half)] = psum_a.tile([P, PACK, HALF], F32, name="bank")
             for t in ts:
@@ -127,8 +127,8 @@ def tile_moe_two_mlp_silu_kernel(
                     out=banks[(e, half)][:, t, :],
                     lhsT=w1_codes[e][o][:, t * P : (t + 1) * P].bitcast(FP8X4),
                     lhsT_scale=w1_scales[e][o][:, t * P : (t + 1) * P],
-                    rhs=slot_words[e][o][:, cols].bitcast(FP8X4),
-                    rhs_scale=slot_scales[e][4 * o : P, cols],
+                    rhs=slot_words[e // 2][o][:, cols].bitcast(FP8X4),
+                    rhs_scale=slot_scales[e // 2][4 * o : P, cols],
                     start=(o == 0 and t == 0),
                     stop=(o == PASSES - 1 and t == PACK - 1),
                 )
@@ -178,125 +178,116 @@ def tile_moe_two_mlp_silu_kernel(
         nc.sync.dma_start(offs_sb[:], offs)
         load_words(0)
         load_scales()
+        load_gate(0)
         load_w1(0, 0)
+        nc.sync.dma_start(dst_sb[:], dst)
         load_words(1)
         load_w1(0, 1)
-        load_w2(0)
         load_w1(1, 0)
         load_w1(1, 1)
-        nc.sync.dma_start(dst_sb[:], dst)
-        load_gate(0)
+        load_w2(0)
         load_w2(1)
-        load_w1(2, 0)
-        load_w1(2, 1)
         load_gate(1)
         load_w2(2)
+        load_w1(2, 0)
+        load_w1(2, 1)
         load_w1(3, 0)
         load_w1(3, 1)
         load_gate(2)
         load_w2(3)
         load_gate(3)
-        gather_words(0, 0)
-        gather_words(1, 0)
-        gather_words(2, 0)
-        gather_words(3, 0)
-        gather_scales(0)
-        gather_scales(1)
+        cast_w1_vector(0, 1)
+        cast_w1_scalar(0, 1)
         cast_w1_scalar(0, 0)
-        cast_w1_vector(0, 0)
         gather_words(0, 1)
-        gather_words(1, 1)
+        cast_w1_vector(0, 0)
         quantise_w1(0, 0, 0, 4)
+        gather_words(2, 0)
+        gather_scales(2)
+        gather_words(0, 0)
+        gather_words(2, 1)
+        gather_scales(0)
         first_layer(0, 0, 0, range(4))
         first_layer(0, 0, 1, range(4))
-        gather_scales(2)
-        gather_scales(3)
-        gather_words(2, 1)
-        cast_w1_scalar(0, 1)
-        cast_w1_vector(0, 1)
         quantise_w1(0, 1, 0, 2)
         first_layer(0, 1, 0, (0, 1))
         first_layer(0, 1, 1, (0, 1))
         quantise_w1(0, 1, 2, 4)
         first_layer(0, 1, 0, (2, 3))
         first_layer(0, 1, 1, (2, 3))
-        gather_words(3, 1)
-        cast_w1_vector(1, 0)
-        cast_w1_scalar(1, 0)
+        cast_w2(0)
         silu(0, 0)
         silu(0, 1)
+        cast_w1_vector(1, 0)
+        cast_w1_scalar(1, 0)
         cast_w1_scalar(1, 1)
-        quantise_w1(1, 0, 0, 4)
         cast_w1_vector(1, 1)
-        cast_w2(0)
-        first_layer(1, 0, 0, range(4))
-        first_layer(1, 0, 1, range(4))
         quantise_h(0, 0, 256)
         quantise_w2(0)
         quantise_w1(1, 1, 0, 2)
-        second_layer(0, 0, 256)
+        quantise_w1(1, 0, 0, 4)
         quantise_w1(1, 1, 2, 4)
-        copy_y(0, 0, 256)
+        first_layer(1, 0, 0, range(4))
+        first_layer(1, 0, 1, range(4))
         first_layer(1, 1, 0, (0, 1))
         first_layer(1, 1, 1, (0, 1))
         first_layer(1, 1, 0, (2, 3))
-        scatter(0, 0, 128)
         first_layer(1, 1, 1, (2, 3))
+        second_layer(0, 0, 256)
+        copy_y(0, 0, 256)
+        cast_w2(1)
+        scatter(0, 0, 256)
+        silu(1, 0)
+        silu(1, 1)
         cast_w1_vector(2, 0)
         cast_w1_scalar(2, 0)
-        silu(1, 0)
-        scatter(0, 128, 256)
-        silu(1, 1)
         cast_w1_scalar(2, 1)
-        quantise_w1(2, 0, 0, 4)
         cast_w1_vector(2, 1)
-        cast_w2(1)
-        first_layer(2, 0, 0, range(4))
-        first_layer(2, 0, 1, range(4))
         quantise_h(1, 0, 256)
         quantise_w2(1)
         quantise_w1(2, 1, 0, 2)
-        second_layer(1, 0, 256)
+        quantise_w1(2, 0, 0, 4)
         quantise_w1(2, 1, 2, 4)
-        copy_y(1, 0, 256)
+        first_layer(2, 0, 0, range(4))
+        first_layer(2, 0, 1, range(4))
         first_layer(2, 1, 0, (0, 1))
         first_layer(2, 1, 1, (0, 1))
         first_layer(2, 1, 0, (2, 3))
-        scatter(1, 0, 128)
         first_layer(2, 1, 1, (2, 3))
+        second_layer(1, 0, 256)
+        copy_y(1, 0, 256)
+        cast_w2(2)
+        scatter(1, 0, 256)
+        silu(2, 0)
+        silu(2, 1)
         cast_w1_vector(3, 0)
         cast_w1_scalar(3, 0)
-        silu(2, 0)
-        scatter(1, 128, 256)
-        silu(2, 1)
         cast_w1_scalar(3, 1)
-        quantise_w1(3, 0, 0, 4)
         cast_w1_vector(3, 1)
-        cast_w2(2)
-        first_layer(3, 0, 0, range(4))
-        first_layer(3, 0, 1, range(4))
         quantise_h(2, 0, 256)
         quantise_w2(2)
         quantise_w1(3, 1, 0, 2)
-        second_layer(2, 0, 256)
+        quantise_w1(3, 0, 0, 4)
         quantise_w1(3, 1, 2, 4)
-        copy_y(2, 0, 256)
+        first_layer(3, 0, 0, range(4))
+        first_layer(3, 0, 1, range(4))
         first_layer(3, 1, 0, (0, 1))
         first_layer(3, 1, 1, (0, 1))
         first_layer(3, 1, 0, (2, 3))
-        scatter(2, 0, 128)
         first_layer(3, 1, 1, (2, 3))
-        cast_w2(3)
-        scatter(2, 128, 256)
+        second_layer(2, 0, 256)
+        copy_y(2, 0, 256)
         silu(3, 0)
+        cast_w2(3)
         silu(3, 1)
-        quantise_w2(3)
         quantise_h(3, 0, 128)
+        scatter(2, 0, 256)
+        quantise_w2(3)
         second_layer(3, 0, 128)
         copy_y(3, 0, 128)
         quantise_h(3, 128, 256)
-        second_layer(3, 128, 256)
         scatter(3, 0, 128)
+        second_layer(3, 128, 256)
         copy_y(3, 128, 256)
         scatter(3, 128, 256)
         nc.sync.dma_start(out=out, in_=out_sb[:])

@@ -22,7 +22,7 @@ PASSES = K // K_PASS
 HALF = C // 2
 LIST_COLS = C // 16
 
-VECTOR_SHARE = [[0,24],[48,80],[64,24],[48,96]]
+VECTOR_SHARE = [[0,16],[8,88],[64,8],[48,88]]
 W2_ON_SCALAR = [0,1,1,1]
 
 
@@ -50,7 +50,7 @@ def tile_moe_two_mlp_silu_kernel(
         w2_bf = [sb("w2_bf%d" % e, [P, N, PACK], BF16) for e in range(E)]
         w2_codes = [sb("w2_codes%d" % e, [P, N], U32) for e in range(E)]
         w2_scales = [sb("w2_scales%d" % e, [P, N], U8) for e in range(E)]
-        gate_sb = [sb("gate_sb%d" % e, [P, C], F32) for e in range(E)]
+        gate_sb = [sb("gate_sb%d" % g, [P, 2 * C], F32) for g in range(E // 2)]
         slot_words = [[sb("slot_words%d_%d" % (g, o), [P, 2 * C], U32) for o in range(PASSES)] for g in range(E // 2)]
         slot_scales = [sb("slot_scales%d" % g, [P, 2 * C], U8) for g in range(E // 2)]
         h_bf = [sb("h_bf%d" % e, [P, C, PACK], BF16) for e in range(E)]
@@ -72,7 +72,7 @@ def tile_moe_two_mlp_silu_kernel(
             nc.sync.dma_start(out=w2_raw[e][:], in_=w2[e].rearrange("(p j) n -> p j n", j=PACK))
 
         def load_gate(e):
-            nc.sync.dma_start(out=gate_sb[e][:], in_=gate[:, e * C : (e + 1) * C])
+            nc.sync.dma_start(out=gate_sb[e][:], in_=gate[:, 2 * e * C : 2 * (e + 1) * C])
 
         def gather_scales(e):
             window = tok_scales[:].bitcast(U8)
@@ -163,7 +163,7 @@ def tile_moe_two_mlp_silu_kernel(
 
         def scatter(e, c0, c1):
             places = dst_sb[:, (e * C + c0) // 16 : (e * C + c1) // 16]
-            nc.vector.tensor_tensor(out_sb[:].indirect(places), y_sb[e][:, c0:c1], gate_sb[e][:, c0:c1], MULT)
+            nc.vector.tensor_tensor(out_sb[:].indirect(places), y_sb[e][:, c0:c1], gate_sb[e // 2][:, (e % 2) * C + c0 : (e % 2) * C + c1], MULT)
 
         def load_scales():
             for q in range(4):
@@ -178,116 +178,114 @@ def tile_moe_two_mlp_silu_kernel(
         nc.sync.dma_start(offs_sb[:], offs)
         load_words(0)
         load_scales()
-        load_gate(0)
         load_w1(0, 0)
-        nc.sync.dma_start(dst_sb[:], dst)
         load_words(1)
+        nc.sync.dma_start(dst_sb[:], dst)
         load_w1(0, 1)
         load_w1(1, 0)
-        load_w1(1, 1)
         load_w2(0)
+        load_w1(1, 1)
         load_w2(1)
-        load_gate(1)
+        load_gate(0)
         load_w2(2)
         load_w1(2, 0)
         load_w1(2, 1)
         load_w1(3, 0)
         load_w1(3, 1)
-        load_gate(2)
+        load_gate(1)
         load_w2(3)
-        load_gate(3)
-        cast_w1_vector(0, 1)
-        cast_w1_scalar(0, 1)
-        cast_w1_scalar(0, 0)
-        gather_words(0, 1)
         cast_w1_vector(0, 0)
-        quantise_w1(0, 0, 0, 4)
-        gather_words(2, 0)
         gather_scales(2)
-        gather_words(0, 0)
+        cast_w1_scalar(0, 1)
         gather_words(2, 1)
+        gather_words(0, 1)
+        cast_w1_vector(0, 1)
+        cast_w1_scalar(0, 0)
         gather_scales(0)
+        gather_words(0, 0)
+        quantise_w1(0, 0, 0, 4)
         first_layer(0, 0, 0, range(4))
         first_layer(0, 0, 1, range(4))
         quantise_w1(0, 1, 0, 2)
+        quantise_w1(0, 1, 2, 4)
+        gather_words(2, 0)
         first_layer(0, 1, 0, (0, 1))
         first_layer(0, 1, 1, (0, 1))
-        quantise_w1(0, 1, 2, 4)
         first_layer(0, 1, 0, (2, 3))
         first_layer(0, 1, 1, (2, 3))
-        cast_w2(0)
         silu(0, 0)
+        cast_w1_vector(1, 1)
+        cast_w1_scalar(1, 1)
         silu(0, 1)
         cast_w1_vector(1, 0)
         cast_w1_scalar(1, 0)
-        cast_w1_scalar(1, 1)
-        cast_w1_vector(1, 1)
-        quantise_h(0, 0, 256)
-        quantise_w2(0)
-        quantise_w1(1, 1, 0, 2)
         quantise_w1(1, 0, 0, 4)
-        quantise_w1(1, 1, 2, 4)
+        quantise_h(0, 0, 256)
+        cast_w2(0)
+        quantise_w1(1, 1, 0, 2)
+        quantise_w2(0)
         first_layer(1, 0, 0, range(4))
         first_layer(1, 0, 1, range(4))
         first_layer(1, 1, 0, (0, 1))
         first_layer(1, 1, 1, (0, 1))
+        quantise_w1(1, 1, 2, 4)
         first_layer(1, 1, 0, (2, 3))
-        first_layer(1, 1, 1, (2, 3))
         second_layer(0, 0, 256)
         copy_y(0, 0, 256)
-        cast_w2(1)
-        scatter(0, 0, 256)
+        first_layer(1, 1, 1, (2, 3))
         silu(1, 0)
+        cast_w1_vector(2, 1)
+        cast_w1_scalar(2, 1)
         silu(1, 1)
         cast_w1_vector(2, 0)
         cast_w1_scalar(2, 0)
-        cast_w1_scalar(2, 1)
-        cast_w1_vector(2, 1)
-        quantise_h(1, 0, 256)
-        quantise_w2(1)
-        quantise_w1(2, 1, 0, 2)
         quantise_w1(2, 0, 0, 4)
-        quantise_w1(2, 1, 2, 4)
+        quantise_h(1, 0, 256)
+        cast_w2(1)
+        quantise_w1(2, 1, 0, 2)
+        quantise_w2(1)
         first_layer(2, 0, 0, range(4))
         first_layer(2, 0, 1, range(4))
         first_layer(2, 1, 0, (0, 1))
         first_layer(2, 1, 1, (0, 1))
+        quantise_w1(2, 1, 2, 4)
         first_layer(2, 1, 0, (2, 3))
-        first_layer(2, 1, 1, (2, 3))
         second_layer(1, 0, 256)
         copy_y(1, 0, 256)
-        cast_w2(2)
-        scatter(1, 0, 256)
+        scatter(0, 0, 256)
+        first_layer(2, 1, 1, (2, 3))
         silu(2, 0)
+        cast_w1_vector(3, 1)
+        cast_w1_scalar(3, 1)
         silu(2, 1)
         cast_w1_vector(3, 0)
         cast_w1_scalar(3, 0)
-        cast_w1_scalar(3, 1)
-        cast_w1_vector(3, 1)
-        quantise_h(2, 0, 256)
-        quantise_w2(2)
-        quantise_w1(3, 1, 0, 2)
         quantise_w1(3, 0, 0, 4)
-        quantise_w1(3, 1, 2, 4)
+        quantise_h(2, 0, 256)
+        cast_w2(2)
+        quantise_w1(3, 1, 0, 2)
+        quantise_w2(2)
         first_layer(3, 0, 0, range(4))
         first_layer(3, 0, 1, range(4))
         first_layer(3, 1, 0, (0, 1))
         first_layer(3, 1, 1, (0, 1))
+        quantise_w1(3, 1, 2, 4)
         first_layer(3, 1, 0, (2, 3))
-        first_layer(3, 1, 1, (2, 3))
         second_layer(2, 0, 256)
         copy_y(2, 0, 256)
-        silu(3, 0)
-        cast_w2(3)
+        scatter(1, 0, 256)
+        first_layer(3, 1, 1, (2, 3))
         silu(3, 1)
+        silu(3, 0)
         quantise_h(3, 0, 128)
+        cast_w2(3)
         scatter(2, 0, 256)
         quantise_w2(3)
-        second_layer(3, 0, 128)
-        copy_y(3, 0, 128)
         quantise_h(3, 128, 256)
-        scatter(3, 0, 128)
+        second_layer(3, 0, 128)
         second_layer(3, 128, 256)
         copy_y(3, 128, 256)
+        copy_y(3, 0, 128)
+        scatter(3, 0, 128)
         scatter(3, 128, 256)
         nc.sync.dma_start(out=out, in_=out_sb[:])

@@ -22,8 +22,8 @@ PASSES = K // K_PASS
 HALF = C // 2
 LIST_COLS = C // 16
 
-VECTOR_SHARE = [[0,16],[8,88],[64,8],[48,88]]
-W2_ON_SCALAR = [0,1,1,1]
+VECTOR_SHARE = [[0,0],[40,96],[64,32],[72,56]]
+W2_ON_SCALAR = [1,1,0,1]
 
 
 def tile_moe_two_mlp_silu_kernel(
@@ -64,6 +64,10 @@ def tile_moe_two_mlp_silu_kernel(
         def load_w1(e, o):
             rows = w1[e, o * K_PASS : (o + 1) * K_PASS, :]
             nc.sync.dma_start(out=w1_raw[e][o][:], in_=rows.rearrange("(p j) c -> p j c", j=PACK))
+
+        def load_w1_columns(e, o, c0, c1):
+            rows = w1[e, o * K_PASS : (o + 1) * K_PASS, c0:c1]
+            nc.sync.dma_start(out=w1_raw[e][o][:, :, c0:c1], in_=rows.rearrange("(p j) c -> p j c", j=PACK))
 
         def load_words(o):
             nc.sync.dma_start(out=tok_words[o][:], in_=x_words[o].rearrange("p t r -> p (t r)").bitcast(I32))
@@ -177,115 +181,116 @@ def tile_moe_two_mlp_silu_kernel(
         nc.scalar.activation(warm_out[:], warm_in[:], SILU)
         nc.sync.dma_start(offs_sb[:], offs)
         load_words(0)
-        load_scales()
-        load_w1(0, 0)
         load_words(1)
-        nc.sync.dma_start(dst_sb[:], dst)
+        load_w1(0, 0)
+        load_scales()
         load_w1(0, 1)
+        nc.sync.dma_start(dst_sb[:], dst)
         load_w1(1, 0)
         load_w2(0)
         load_w1(1, 1)
         load_w2(1)
         load_gate(0)
-        load_w2(2)
         load_w1(2, 0)
         load_w1(2, 1)
         load_w1(3, 0)
-        load_w1(3, 1)
-        load_gate(1)
+        load_w2(2)
+        load_w1_columns(3, 1, PACK * VECTOR_SHARE[3][1], H)
+        load_w1_columns(3, 1, 0, PACK * VECTOR_SHARE[3][1])
         load_w2(3)
+        load_gate(1)
         cast_w1_vector(0, 0)
-        gather_scales(2)
-        cast_w1_scalar(0, 1)
-        gather_words(2, 1)
         gather_words(0, 1)
-        cast_w1_vector(0, 1)
-        cast_w1_scalar(0, 0)
         gather_scales(0)
+        cast_w1_scalar(0, 0)
         gather_words(0, 0)
+        cast_w1_vector(0, 1)
+        cast_w1_scalar(0, 1)
+        gather_words(2, 0)
+        quantise_w1(0, 1, 2, 4)
+        gather_words(2, 1)
         quantise_w1(0, 0, 0, 4)
+        gather_scales(2)
+        quantise_w1(0, 1, 0, 2)
         first_layer(0, 0, 0, range(4))
         first_layer(0, 0, 1, range(4))
-        quantise_w1(0, 1, 0, 2)
-        quantise_w1(0, 1, 2, 4)
-        gather_words(2, 0)
         first_layer(0, 1, 0, (0, 1))
         first_layer(0, 1, 1, (0, 1))
         first_layer(0, 1, 0, (2, 3))
         first_layer(0, 1, 1, (2, 3))
-        silu(0, 0)
-        cast_w1_vector(1, 1)
-        cast_w1_scalar(1, 1)
-        silu(0, 1)
-        cast_w1_vector(1, 0)
         cast_w1_scalar(1, 0)
-        quantise_w1(1, 0, 0, 4)
-        quantise_h(0, 0, 256)
         cast_w2(0)
-        quantise_w1(1, 1, 0, 2)
+        cast_w1_scalar(1, 1)
+        cast_w1_vector(1, 0)
+        silu(0, 0)
+        quantise_w1(1, 0, 0, 4)
+        silu(0, 1)
         quantise_w2(0)
+        quantise_h(0, 0, 256)
         first_layer(1, 0, 0, range(4))
         first_layer(1, 0, 1, range(4))
+        second_layer(0, 0, 256)
+        cast_w1_vector(1, 1)
+        quantise_w1(1, 1, 0, 2)
         first_layer(1, 1, 0, (0, 1))
         first_layer(1, 1, 1, (0, 1))
         quantise_w1(1, 1, 2, 4)
-        first_layer(1, 1, 0, (2, 3))
-        second_layer(0, 0, 256)
         copy_y(0, 0, 256)
+        first_layer(1, 1, 0, (2, 3))
         first_layer(1, 1, 1, (2, 3))
-        silu(1, 0)
-        cast_w1_vector(2, 1)
-        cast_w1_scalar(2, 1)
-        silu(1, 1)
-        cast_w1_vector(2, 0)
         cast_w1_scalar(2, 0)
-        quantise_w1(2, 0, 0, 4)
-        quantise_h(1, 0, 256)
         cast_w2(1)
-        quantise_w1(2, 1, 0, 2)
+        cast_w1_scalar(2, 1)
+        cast_w1_vector(2, 0)
+        silu(1, 0)
+        quantise_w1(2, 0, 0, 4)
+        silu(1, 1)
         quantise_w2(1)
+        quantise_h(1, 0, 256)
         first_layer(2, 0, 0, range(4))
         first_layer(2, 0, 1, range(4))
+        second_layer(1, 0, 256)
+        cast_w1_vector(2, 1)
+        quantise_w1(2, 1, 0, 2)
         first_layer(2, 1, 0, (0, 1))
         first_layer(2, 1, 1, (0, 1))
         quantise_w1(2, 1, 2, 4)
-        first_layer(2, 1, 0, (2, 3))
-        second_layer(1, 0, 256)
         copy_y(1, 0, 256)
+        first_layer(2, 1, 0, (2, 3))
         scatter(0, 0, 256)
         first_layer(2, 1, 1, (2, 3))
-        silu(2, 0)
-        cast_w1_vector(3, 1)
-        cast_w1_scalar(3, 1)
-        silu(2, 1)
-        cast_w1_vector(3, 0)
         cast_w1_scalar(3, 0)
-        quantise_w1(3, 0, 0, 4)
-        quantise_h(2, 0, 256)
         cast_w2(2)
-        quantise_w1(3, 1, 0, 2)
+        cast_w1_scalar(3, 1)
+        cast_w1_vector(3, 0)
+        silu(2, 0)
+        quantise_w1(3, 0, 0, 4)
+        silu(2, 1)
         quantise_w2(2)
+        quantise_h(2, 0, 256)
         first_layer(3, 0, 0, range(4))
         first_layer(3, 0, 1, range(4))
+        second_layer(2, 0, 256)
+        cast_w1_vector(3, 1)
+        quantise_w1(3, 1, 0, 2)
         first_layer(3, 1, 0, (0, 1))
         first_layer(3, 1, 1, (0, 1))
         quantise_w1(3, 1, 2, 4)
-        first_layer(3, 1, 0, (2, 3))
-        second_layer(2, 0, 256)
         copy_y(2, 0, 256)
+        first_layer(3, 1, 0, (2, 3))
         scatter(1, 0, 256)
         first_layer(3, 1, 1, (2, 3))
+        scatter(2, 0, 256)
+        cast_w2(3)
+        quantise_w2(3)
         silu(3, 1)
         silu(3, 0)
-        quantise_h(3, 0, 128)
-        cast_w2(3)
-        scatter(2, 0, 256)
-        quantise_w2(3)
         quantise_h(3, 128, 256)
+        quantise_h(3, 0, 128)
         second_layer(3, 0, 128)
-        second_layer(3, 128, 256)
-        copy_y(3, 128, 256)
         copy_y(3, 0, 128)
         scatter(3, 0, 128)
+        second_layer(3, 128, 256)
+        copy_y(3, 128, 256)
         scatter(3, 128, 256)
         nc.sync.dma_start(out=out, in_=out_sb[:])

@@ -22,8 +22,9 @@ PASSES = K // K_PASS
 HALF = C // 2
 LIST_COLS = C // 16
 
-VECTOR_SHARE = [[0,0],[40,96],[64,32],[72,56]]
-W2_ON_SCALAR = [1,1,0,1]
+FIRST = 72
+VECTOR_SHARE = 40
+LAST_SHARE = 36
 
 
 def tile_moe_two_mlp_silu_kernel(
@@ -32,17 +33,26 @@ def tile_moe_two_mlp_silu_kernel(
     nc = tc.nc
     with ExitStack() as ctx:
         keep = ctx.enter_context(tc.tile_pool(name="keep", bufs=1))
+        stage = ctx.enter_context(tc.tile_pool(name="stage", bufs=1))
         psum_a = ctx.enter_context(tc.psum_pool(name="psum_a", bufs=6))
         psum_y = ctx.enter_context(tc.psum_pool(name="psum_y", bufs=2))
 
-        def sb(name, shape, dtype):
-            return keep.tile(shape, dtype, name=name, align_bytes=64)
+        def sb(name, shape, dtype, tag=""):
+            return keep.tile(shape, dtype, name=name, tag=tag or name, align_bytes=64)
 
+        def staged(name, shape, dtype, e, o, skip=0):
+            offset = (e * PASSES + o) * PACK * H * 4 + skip
+            return stage.tile(shape, dtype, name=name, align_bytes=64, offset=offset)
+
+        pieces = ((0, FIRST), (FIRST, P))
         offs_sb = keep.tile([P, E * LIST_COLS], U16, name="offs_sb")
         dst_sb = keep.tile([P, E * LIST_COLS], U16, name="dst_sb")
         tok_scales = sb("tok_scales", [P, T // 4], I32)
         tok_words = [sb("tok_words%d" % o, [P, T], I32) for o in range(PASSES)]
-        w1_raw = [[sb("w1_raw%d_%d" % (e, o), [P, PACK, H], F32) for o in range(PASSES)] for e in range(E)]
+        w1_raw = [
+            [[staged("w1_raw%d_%d_%d" % (e, o, s), [P, PACK, PACK * (m1 - m0)], F32, e, o, PACK * PACK * m0 * 4) for s, (m0, m1) in enumerate(pieces)] for o in range(PASSES)]
+            for e in range(E)
+        ]
         w1_bf = [[sb("w1_bf%d_%d" % (e, o), [P, PACK, P, PACK], BF16) for o in range(PASSES)] for e in range(E)]
         w1_codes = [[sb("w1_codes%d_%d" % (e, o), [P, H], U32) for o in range(PASSES)] for e in range(E)]
         w1_scales = [[sb("w1_scales%d_%d" % (e, o), [P, H], U8) for o in range(PASSES)] for e in range(E)]
@@ -50,24 +60,29 @@ def tile_moe_two_mlp_silu_kernel(
         w2_bf = [sb("w2_bf%d" % e, [P, N, PACK], BF16) for e in range(E)]
         w2_codes = [sb("w2_codes%d" % e, [P, N], U32) for e in range(E)]
         w2_scales = [sb("w2_scales%d" % e, [P, N], U8) for e in range(E)]
-        gate_sb = [sb("gate_sb%d" % g, [P, 2 * C], F32) for g in range(E // 2)]
-        slot_words = [[sb("slot_words%d_%d" % (g, o), [P, 2 * C], U32) for o in range(PASSES)] for g in range(E // 2)]
-        slot_scales = [sb("slot_scales%d" % g, [P, 2 * C], U8) for g in range(E // 2)]
-        h_bf = [sb("h_bf%d" % e, [P, C, PACK], BF16) for e in range(E)]
-        h_codes = [sb("h_codes%d" % e, [P, C], U32) for e in range(E)]
+        gate_sb = [sb("gate_sb%d" % e, [P, C], F32) for e in range(E)]
+        slot_words = [sb("slot_words%d" % o, [P, E * C], U32) for o in range(PASSES)]
+        slot_scales = sb("slot_scales", [P, E * C], U8)
+        h_bf = [staged("h_bf%d" % e, [P, C, PACK], BF16, e + 1, 0) for e in range(E - 1)]
+        h_bf.append(sb("h_bf%d" % (E - 1), [P, C, PACK], BF16))
+        h_codes = [staged("h_codes%d" % e, [P, C], U32, e + 1, 1) for e in range(E - 2)]
+        h_codes.extend(sb("h_codes%d" % e, [P, C], U32) for e in range(E - 2, E))
         h_scales = [sb("h_scales%d" % e, [P, C], U8) for e in range(E)]
-        y_sb = [sb("y_sb%d" % e, [P, C], F32) for e in range(E)]
+        y_sb = [staged("y_sb%d" % e, [P, C], F32, e + 2, 0, 2048) for e in range(E - 2)]
+        y_sb.append(staged("y_sb%d" % (E - 2), [P, C], F32, E - 1, 1))
+        y_sb.append(sb("y_sb%d" % (E - 1), [P, C], F32))
         out_sb = sb("out_sb", [P, T], F32)
         warm_in = sb("warm_in", [P, 16], F32)
         warm_out = sb("warm_out", [P, 16], F32)
 
-        def load_w1(e, o):
-            rows = w1[e, o * K_PASS : (o + 1) * K_PASS, :]
-            nc.sync.dma_start(out=w1_raw[e][o][:], in_=rows.rearrange("(p j) c -> p j c", j=PACK))
+        def load_w1_piece(e, o, s):
+            m0, m1 = pieces[s]
+            rows = w1[e, o * K_PASS : (o + 1) * K_PASS, PACK * m0 : PACK * m1]
+            nc.sync.dma_start(out=w1_raw[e][o][s][:], in_=rows.rearrange("(p j) c -> p j c", j=PACK))
 
-        def load_w1_columns(e, o, c0, c1):
-            rows = w1[e, o * K_PASS : (o + 1) * K_PASS, c0:c1]
-            nc.sync.dma_start(out=w1_raw[e][o][:, :, c0:c1], in_=rows.rearrange("(p j) c -> p j c", j=PACK))
+        def load_w1(e, o):
+            load_w1_piece(e, o, 0)
+            load_w1_piece(e, o, 1)
 
         def load_words(o):
             nc.sync.dma_start(out=tok_words[o][:], in_=x_words[o].rearrange("p t r -> p (t r)").bitcast(I32))
@@ -76,28 +91,35 @@ def tile_moe_two_mlp_silu_kernel(
             nc.sync.dma_start(out=w2_raw[e][:], in_=w2[e].rearrange("(p j) n -> p j n", j=PACK))
 
         def load_gate(e):
-            nc.sync.dma_start(out=gate_sb[e][:], in_=gate[:, 2 * e * C : 2 * (e + 1) * C])
+            nc.sync.dma_start(out=gate_sb[e][:], in_=gate[:, e * C : (e + 1) * C])
 
-        def gather_scales(e):
-            window = tok_scales[:].bitcast(U8)
-            nc.vector.tensor_copy(slot_scales[e // 2][:], window.indirect(offs_sb[:, e * LIST_COLS : (e + 2) * LIST_COLS]))
+        def load_scales():
+            for q in range(4):
+                nc.sync.dma_start(
+                    out=tok_scales[32 * q : 32 * q + 4 * PASSES, :],
+                    in_=x_scales[:, 4 * q : 4 * q + 4, :].bitcast(I32),
+                )
 
-        def gather_words(e, o):
-            window = tok_words[o][:].bitcast(U32)
-            nc.vector.tensor_copy(slot_words[e // 2][o][:], window.indirect(offs_sb[:, e * LIST_COLS : (e + 2) * LIST_COLS]))
+        def gather_scales(e0, e1):
+            entries = offs_sb[:, e0 * LIST_COLS : e1 * LIST_COLS]
+            nc.vector.tensor_copy(slot_scales[:, e0 * C : e1 * C], tok_scales[:].bitcast(U8).indirect(entries))
 
-        def cast_w1_part(copy, e, o, m0, m1):
+        def gather_words(o, e0, e1):
+            entries = offs_sb[:, e0 * LIST_COLS : e1 * LIST_COLS]
+            nc.vector.tensor_copy(slot_words[o][:, e0 * C : e1 * C], tok_words[o][:].bitcast(U32).indirect(entries))
+
+        def cast_w1(copy, e, o, s, m0, m1):
+            base = pieces[s][0]
             copy(
                 w1_bf[e][o][:, :, m0:m1, :].rearrange("p t m j -> p m j t"),
-                w1_raw[e][o][:, :, PACK * m0 : PACK * m1].rearrange("p j (m t) -> p m j t", t=PACK),
+                w1_raw[e][o][s][:, :, PACK * (m0 - base) : PACK * (m1 - base)].rearrange("p j (m t) -> p m j t", t=PACK),
             )
 
-        def cast_w1_scalar(e, o):
-            cast_w1_part(nc.scalar.copy, e, o, VECTOR_SHARE[e][o], P)
-
-        def cast_w1_vector(e, o):
-            if VECTOR_SHARE[e][o]:
-                cast_w1_part(nc.vector.tensor_copy, e, o, 0, VECTOR_SHARE[e][o])
+        def cast_block(e, o, share):
+            cast_w1(nc.scalar.copy, e, o, 0, 0, FIRST)
+            cast_w1(nc.scalar.copy, e, o, 1, FIRST + share, P)
+            if share:
+                cast_w1(nc.vector.tensor_copy, e, o, 1, FIRST, FIRST + share)
 
         def quantise_w1(e, o, t0, t1):
             nc.vector.quantize_mx(
@@ -106,8 +128,7 @@ def tile_moe_two_mlp_silu_kernel(
                 in_=w1_bf[e][o][:, t0:t1, :, :].rearrange("p t m j -> p (t m j)"),
             )
 
-        def cast_w2(e):
-            copy = nc.scalar.copy if W2_ON_SCALAR[e] else nc.vector.tensor_copy
+        def cast_w2(copy, e):
             copy(
                 w2_bf[e][:].rearrange("p (c i) j -> p c j i", i=4),
                 w2_raw[e][:].rearrange("p j (c i) -> p c j i", i=4),
@@ -122,38 +143,36 @@ def tile_moe_two_mlp_silu_kernel(
 
         banks = {}
 
-        def first_layer(e, o, half, ts):
-            cols = slice((e % 2) * C + half * HALF, (e % 2) * C + (half + 1) * HALF)
-            if (e, half) not in banks:
-                banks[(e, half)] = psum_a.tile([P, PACK, HALF], F32, name="bank")
-            for t in ts:
-                nc.tensor.matmul_mx(
-                    out=banks[(e, half)][:, t, :],
-                    lhsT=w1_codes[e][o][:, t * P : (t + 1) * P].bitcast(FP8X4),
-                    lhsT_scale=w1_scales[e][o][:, t * P : (t + 1) * P],
-                    rhs=slot_words[e // 2][o][:, cols].bitcast(FP8X4),
-                    rhs_scale=slot_scales[e // 2][4 * o : P, cols],
-                    start=(o == 0 and t == 0),
-                    stop=(o == PASSES - 1 and t == PACK - 1),
-                )
+        def first_layer(e, o, ts):
+            for half in range(2):
+                cols = slice(e * C + half * HALF, e * C + (half + 1) * HALF)
+                if (e, half) not in banks:
+                    banks[(e, half)] = psum_a.tile([P, PACK, HALF], F32, name="bank")
+                for t in ts:
+                    nc.tensor.matmul_mx(
+                        out=banks[(e, half)][:, t, :],
+                        lhsT=w1_codes[e][o][:, t * P : (t + 1) * P].bitcast(FP8X4),
+                        lhsT_scale=w1_scales[e][o][:, t * P : (t + 1) * P],
+                        rhs=slot_words[o][:, cols].bitcast(FP8X4),
+                        rhs_scale=slot_scales[4 * o : P, cols],
+                        start=(o == 0 and t == 0),
+                        stop=(o == PASSES - 1 and t == PACK - 1),
+                    )
 
-        def silu(e, half):
-            cols = slice(half * HALF, (half + 1) * HALF)
-            nc.scalar.activation(h_bf[e][:, cols, :], banks[(e, half)][:].rearrange("p t n -> p n t"), SILU)
+        def silu(e):
+            for half in range(2):
+                cols = slice(half * HALF, (half + 1) * HALF)
+                nc.scalar.activation(h_bf[e][:, cols, :], banks[(e, half)][:].rearrange("p t n -> p n t"), SILU)
 
-        def quantise_h(e, c0, c1):
+        def second_layer(e, c0, c1):
             nc.vector.quantize_mx(
                 out=h_codes[e][:, c0:c1].bitcast(FP8X4),
                 scales=h_scales[e][:, c0:c1],
                 in_=h_bf[e][:, c0:c1, :].rearrange("p n t -> p (n t)"),
             )
-
-        y_banks = {}
-
-        def second_layer(e, c0, c1):
-            y_banks[(e, c0)] = psum_y.tile([P, c1 - c0], F32, name="y_ps")
+            y_ps = psum_y.tile([P, c1 - c0], F32, name="y_ps")
             nc.tensor.matmul_mx(
-                out=y_banks[(e, c0)][:],
+                out=y_ps[:],
                 lhsT=w2_codes[e][:].bitcast(FP8X4),
                 lhsT_scale=w2_scales[e][:],
                 rhs=h_codes[e][:, c0:c1].bitcast(FP8X4),
@@ -161,136 +180,66 @@ def tile_moe_two_mlp_silu_kernel(
                 start=True,
                 stop=True,
             )
+            return y_ps
 
-        def copy_y(e, c0, c1):
-            nc.scalar.copy(y_sb[e][:, c0:c1], y_banks[(e, c0)][:])
-
-        def scatter(e, c0, c1):
+        def scatter(e, c0, c1, y_ps):
+            nc.scalar.copy(y_sb[e][:, c0:c1], y_ps[:])
             places = dst_sb[:, (e * C + c0) // 16 : (e * C + c1) // 16]
-            nc.vector.tensor_tensor(out_sb[:].indirect(places), y_sb[e][:, c0:c1], gate_sb[e // 2][:, (e % 2) * C + c0 : (e % 2) * C + c1], MULT)
+            nc.vector.tensor_tensor(out_sb[:].indirect(places), y_sb[e][:, c0:c1], gate_sb[e][:, c0:c1], MULT)
 
-        def load_scales():
-            for q in range(4):
-                nc.sync.dma_start(
-                    out=tok_scales[32 * q : 32 * q + 4 * PASSES, :],
-                    in_=x_scales[:, 4 * q : 4 * q + 4, :].bitcast(I32),
-                )
-
-        nc.vector.memset(tok_scales[:], 0)
+        nc.gpsimd.memset(tok_scales[:], 0)
         nc.gpsimd.memset(warm_in[:], 0.0)
         nc.scalar.activation(warm_out[:], warm_in[:], SILU)
         nc.sync.dma_start(offs_sb[:], offs)
-        load_words(0)
-        load_words(1)
-        load_w1(0, 0)
+        load_w1_piece(0, 0, 0)
         load_scales()
+        load_w1_piece(0, 0, 1)
+        load_words(0)
         load_w1(0, 1)
-        nc.sync.dma_start(dst_sb[:], dst)
-        load_w1(1, 0)
-        load_w2(0)
-        load_w1(1, 1)
-        load_w2(1)
-        load_gate(0)
-        load_w1(2, 0)
-        load_w1(2, 1)
-        load_w1(3, 0)
-        load_w2(2)
-        load_w1_columns(3, 1, PACK * VECTOR_SHARE[3][1], H)
-        load_w1_columns(3, 1, 0, PACK * VECTOR_SHARE[3][1])
-        load_w2(3)
-        load_gate(1)
-        cast_w1_vector(0, 0)
-        gather_words(0, 1)
-        gather_scales(0)
-        cast_w1_scalar(0, 0)
-        gather_words(0, 0)
-        cast_w1_vector(0, 1)
-        cast_w1_scalar(0, 1)
-        gather_words(2, 0)
-        quantise_w1(0, 1, 2, 4)
-        gather_words(2, 1)
-        quantise_w1(0, 0, 0, 4)
-        gather_scales(2)
-        quantise_w1(0, 1, 0, 2)
-        first_layer(0, 0, 0, range(4))
-        first_layer(0, 0, 1, range(4))
-        first_layer(0, 1, 0, (0, 1))
-        first_layer(0, 1, 1, (0, 1))
-        first_layer(0, 1, 0, (2, 3))
-        first_layer(0, 1, 1, (2, 3))
-        cast_w1_scalar(1, 0)
-        cast_w2(0)
-        cast_w1_scalar(1, 1)
-        cast_w1_vector(1, 0)
-        silu(0, 0)
-        quantise_w1(1, 0, 0, 4)
-        silu(0, 1)
-        quantise_w2(0)
-        quantise_h(0, 0, 256)
-        first_layer(1, 0, 0, range(4))
-        first_layer(1, 0, 1, range(4))
-        second_layer(0, 0, 256)
-        cast_w1_vector(1, 1)
-        quantise_w1(1, 1, 0, 2)
-        first_layer(1, 1, 0, (0, 1))
-        first_layer(1, 1, 1, (0, 1))
-        quantise_w1(1, 1, 2, 4)
-        copy_y(0, 0, 256)
-        first_layer(1, 1, 0, (2, 3))
-        first_layer(1, 1, 1, (2, 3))
-        cast_w1_scalar(2, 0)
-        cast_w2(1)
-        cast_w1_scalar(2, 1)
-        cast_w1_vector(2, 0)
-        silu(1, 0)
-        quantise_w1(2, 0, 0, 4)
-        silu(1, 1)
-        quantise_w2(1)
-        quantise_h(1, 0, 256)
-        first_layer(2, 0, 0, range(4))
-        first_layer(2, 0, 1, range(4))
-        second_layer(1, 0, 256)
-        cast_w1_vector(2, 1)
-        quantise_w1(2, 1, 0, 2)
-        first_layer(2, 1, 0, (0, 1))
-        first_layer(2, 1, 1, (0, 1))
-        quantise_w1(2, 1, 2, 4)
-        copy_y(1, 0, 256)
-        first_layer(2, 1, 0, (2, 3))
-        scatter(0, 0, 256)
-        first_layer(2, 1, 1, (2, 3))
-        cast_w1_scalar(3, 0)
-        cast_w2(2)
-        cast_w1_scalar(3, 1)
-        cast_w1_vector(3, 0)
-        silu(2, 0)
-        quantise_w1(3, 0, 0, 4)
-        silu(2, 1)
-        quantise_w2(2)
-        quantise_h(2, 0, 256)
-        first_layer(3, 0, 0, range(4))
-        first_layer(3, 0, 1, range(4))
-        second_layer(2, 0, 256)
-        cast_w1_vector(3, 1)
-        quantise_w1(3, 1, 0, 2)
-        first_layer(3, 1, 0, (0, 1))
-        first_layer(3, 1, 1, (0, 1))
-        quantise_w1(3, 1, 2, 4)
-        copy_y(2, 0, 256)
-        first_layer(3, 1, 0, (2, 3))
-        scatter(1, 0, 256)
-        first_layer(3, 1, 1, (2, 3))
-        scatter(2, 0, 256)
-        cast_w2(3)
-        quantise_w2(3)
-        silu(3, 1)
-        silu(3, 0)
-        quantise_h(3, 128, 256)
-        quantise_h(3, 0, 128)
-        second_layer(3, 0, 128)
-        copy_y(3, 0, 128)
-        scatter(3, 0, 128)
-        second_layer(3, 128, 256)
-        copy_y(3, 128, 256)
-        scatter(3, 128, 256)
+        load_words(1)
+        for e in range(1, E):
+            if e > 1:
+                load_w2(e - 1)
+            load_w1(e, 0)
+            if e == 1:
+                load_w2(0)
+                nc.sync.dma_start(dst_sb[:], dst)
+            else:
+                load_gate(e - 2)
+            load_w1(e, 1)
+        load_w2(E - 1)
+        load_gate(E - 2)
+        load_gate(E - 1)
+
+        gather_scales(0, 1)
+        gather_scales(1, E)
+        for o in range(PASSES):
+            cast_block(0, o, 0)
+            gather_words(o, 0, 1)
+            quantise_w1(0, o, 0, PACK)
+            first_layer(0, o, range(PACK))
+            gather_words(o, 1, E)
+        y_ps = None
+        for e in range(1, E):
+            last = e == E - 1
+            cast_w2(nc.vector.tensor_copy, e - 1)
+            cast_block(e, 0, VECTOR_SHARE if e > 1 else 0)
+            quantise_w2(e - 1)
+            quantise_w1(e, 0, 0, PACK)
+            first_layer(e, 0, range(PACK))
+            if e > 1:
+                scatter(e - 2, 0, C, y_ps)
+            silu(e - 1)
+            cast_block(e, 1, LAST_SHARE if last else VECTOR_SHARE)
+            y_ps = second_layer(e - 1, 0, C)
+            quantise_w1(e, 1, 0, 2)
+            quantise_w1(e, 1, 2, PACK)
+            first_layer(e, 1, range(PACK))
+        scatter(E - 2, 0, C, y_ps)
+        cast_w2(nc.scalar.copy, E - 1)
+        quantise_w2(E - 1)
+        silu(E - 1)
+        y_halves = [second_layer(E - 1, half * HALF, (half + 1) * HALF) for half in range(2)]
+        for half in range(2):
+            scatter(E - 1, half * HALF, (half + 1) * HALF, y_halves[half])
         nc.sync.dma_start(out=out, in_=out_sb[:])

@@ -22,9 +22,9 @@ PASSES = K // K_PASS
 HALF = C // 2
 LIST_COLS = C // 16
 
-FIRST = 72
-VECTOR_SHARE = 40
-LAST_SHARE = 36
+VECTOR_SHARE = 44
+LEAD = 240
+LAST_SHARE = 42
 
 
 def tile_moe_two_mlp_silu_kernel(
@@ -33,26 +33,19 @@ def tile_moe_two_mlp_silu_kernel(
     nc = tc.nc
     with ExitStack() as ctx:
         keep = ctx.enter_context(tc.tile_pool(name="keep", bufs=1))
-        stage = ctx.enter_context(tc.tile_pool(name="stage", bufs=1))
         psum_a = ctx.enter_context(tc.psum_pool(name="psum_a", bufs=6))
         psum_y = ctx.enter_context(tc.psum_pool(name="psum_y", bufs=2))
 
         def sb(name, shape, dtype, tag=""):
             return keep.tile(shape, dtype, name=name, tag=tag or name, align_bytes=64)
 
-        def staged(name, shape, dtype, e, o, skip=0):
-            offset = (e * PASSES + o) * PACK * H * 4 + skip
-            return stage.tile(shape, dtype, name=name, align_bytes=64, offset=offset)
-
-        pieces = ((0, FIRST), (FIRST, P))
         offs_sb = keep.tile([P, E * LIST_COLS], U16, name="offs_sb")
         dst_sb = keep.tile([P, E * LIST_COLS], U16, name="dst_sb")
         tok_scales = sb("tok_scales", [P, T // 4], I32)
         tok_words = [sb("tok_words%d" % o, [P, T], I32) for o in range(PASSES)]
-        w1_raw = [
-            [[staged("w1_raw%d_%d_%d" % (e, o, s), [P, PACK, PACK * (m1 - m0)], F32, e, o, PACK * PACK * m0 * 4) for s, (m0, m1) in enumerate(pieces)] for o in range(PASSES)]
-            for e in range(E)
-        ]
+        stage = [[sb("stage%d_%d" % (e, o), [P, LEAD + PACK * H // 2], F32) for o in range(PASSES)] for e in range(E)]
+        w1_low = [[stage[e][o][:, LEAD:].rearrange("p (j c) -> p j c", j=PACK) for o in range(PASSES)] for e in range(E)]
+        w1_high = [[sb("w1_high%d_%d" % (e, o), [P, PACK, H // 2], F32) for o in range(PASSES)] for e in range(E)]
         w1_bf = [[sb("w1_bf%d_%d" % (e, o), [P, PACK, P, PACK], BF16) for o in range(PASSES)] for e in range(E)]
         w1_codes = [[sb("w1_codes%d_%d" % (e, o), [P, H], U32) for o in range(PASSES)] for e in range(E)]
         w1_scales = [[sb("w1_scales%d_%d" % (e, o), [P, H], U8) for o in range(PASSES)] for e in range(E)]
@@ -63,26 +56,27 @@ def tile_moe_two_mlp_silu_kernel(
         gate_sb = [sb("gate_sb%d" % e, [P, C], F32) for e in range(E)]
         slot_words = [sb("slot_words%d" % o, [P, E * C], U32) for o in range(PASSES)]
         slot_scales = sb("slot_scales", [P, E * C], U8)
-        h_bf = [staged("h_bf%d" % e, [P, C, PACK], BF16, e + 1, 0) for e in range(E - 1)]
-        h_bf.append(sb("h_bf%d" % (E - 1), [P, C, PACK], BF16))
-        h_codes = [staged("h_codes%d" % e, [P, C], U32, e + 1, 1) for e in range(E - 2)]
-        h_codes.extend(sb("h_codes%d" % e, [P, C], U32) for e in range(E - 2, E))
+        h_bf = [
+            stage[e + 1][0][:, LEAD + 2 * C :].bitcast(BF16).rearrange("p (n t) -> p n t", t=PACK) for e in range(E - 1)
+        ]
+        h_bf[0] = w1_high[1][0][:, 0:2, :].rearrange("p j c -> p (j c)").bitcast(BF16).rearrange("p (n t) -> p n t", t=PACK)
+        h_bf.append(sb("h_bf", [P, C, PACK], BF16))
+        h_codes = [sb("h_codes%d" % e, [P, C], U32) for e in range(E)]
         h_scales = [sb("h_scales%d" % e, [P, C], U8) for e in range(E)]
-        y_sb = [staged("y_sb%d" % e, [P, C], F32, e + 2, 0, 2048) for e in range(E - 2)]
-        y_sb.append(staged("y_sb%d" % (E - 2), [P, C], F32, E - 1, 1))
-        y_sb.append(sb("y_sb%d" % (E - 1), [P, C], F32))
+        y_sb = [stage[e + 2][0][:, 0:C] for e in range(E - 2)]
+        y_sb.append(w1_high[E - 1][1][:, 0, :])
+        y_sb.append(sb("y_sb", [P, C], F32))
         out_sb = sb("out_sb", [P, T], F32)
         warm_in = sb("warm_in", [P, 16], F32)
         warm_out = sb("warm_out", [P, 16], F32)
 
-        def load_w1_piece(e, o, s):
-            m0, m1 = pieces[s]
-            rows = w1[e, o * K_PASS : (o + 1) * K_PASS, PACK * m0 : PACK * m1]
-            nc.sync.dma_start(out=w1_raw[e][o][s][:], in_=rows.rearrange("(p j) c -> p j c", j=PACK))
+        def load_w1_half(e, o, s):
+            rows = w1[e, o * K_PASS : (o + 1) * K_PASS, s * H // 2 : (s + 1) * H // 2]
+            nc.sync.dma_start(out=(w1_low, w1_high)[s][e][o][:], in_=rows.rearrange("(p j) c -> p j c", j=PACK))
 
         def load_w1(e, o):
-            load_w1_piece(e, o, 0)
-            load_w1_piece(e, o, 1)
+            load_w1_half(e, o, 0)
+            load_w1_half(e, o, 1)
 
         def load_words(o):
             nc.sync.dma_start(out=tok_words[o][:], in_=x_words[o].rearrange("p t r -> p (t r)").bitcast(I32))
@@ -108,18 +102,25 @@ def tile_moe_two_mlp_silu_kernel(
             entries = offs_sb[:, e0 * LIST_COLS : e1 * LIST_COLS]
             nc.vector.tensor_copy(slot_words[o][:, e0 * C : e1 * C], tok_words[o][:].bitcast(U32).indirect(entries))
 
-        def cast_w1(copy, e, o, s, m0, m1):
-            base = pieces[s][0]
+        def cast_w1(copy, e, o, m0, m1):
+            raw, base = (w1_low[e][o], 0) if m0 < P // 2 else (w1_high[e][o], P // 2)
             copy(
                 w1_bf[e][o][:, :, m0:m1, :].rearrange("p t m j -> p m j t"),
-                w1_raw[e][o][s][:, :, PACK * (m0 - base) : PACK * (m1 - base)].rearrange("p j (m t) -> p m j t", t=PACK),
+                raw[:, :, PACK * (m0 - base) : PACK * (m1 - base)].rearrange("p j (m t) -> p m j t", t=PACK),
             )
 
-        def cast_block(e, o, share):
-            cast_w1(nc.scalar.copy, e, o, 0, 0, FIRST)
-            cast_w1(nc.scalar.copy, e, o, 1, FIRST + share, P)
+        def cast_high(e, o, share):
+            cast_w1(nc.scalar.copy, e, o, P // 2, P - share)
             if share:
-                cast_w1(nc.vector.tensor_copy, e, o, 1, FIRST, FIRST + share)
+                cast_w1(nc.vector.tensor_copy, e, o, P - share, P)
+
+        def cast_block(e, o, share):
+            if o == 0 and e > 1:
+                cast_w1(nc.scalar.copy, e, o, 0, P // 4)
+                cast_w1(nc.scalar.copy, e, o, P // 4, P // 2)
+            else:
+                cast_w1(nc.scalar.copy, e, o, 0, P // 2)
+            cast_high(e, o, share)
 
         def quantise_w1(e, o, t0, t1):
             nc.vector.quantize_mx(
@@ -191,18 +192,19 @@ def tile_moe_two_mlp_silu_kernel(
         nc.gpsimd.memset(warm_in[:], 0.0)
         nc.scalar.activation(warm_out[:], warm_in[:], SILU)
         nc.sync.dma_start(offs_sb[:], offs)
-        load_w1_piece(0, 0, 0)
+        load_w1_half(0, 0, 0)
         load_scales()
-        load_w1_piece(0, 0, 1)
+        load_w1_half(0, 0, 1)
+        load_w1_half(0, 1, 0)
         load_words(0)
-        load_w1(0, 1)
-        load_words(1)
+        load_w1_half(0, 1, 1)
         for e in range(1, E):
-            if e > 1:
-                load_w2(e - 1)
-            load_w1(e, 0)
+            load_w1_half(e, 0, 0)
             if e == 1:
-                load_w2(0)
+                load_words(1)
+            load_w1_half(e, 0, 1)
+            load_w2(e - 1)
+            if e == 1:
                 nc.sync.dma_start(dst_sb[:], dst)
             else:
                 load_gate(e - 2)

@@ -1,6 +1,7 @@
 from contextlib import ExitStack
 
 import concourse.mybir as mybir
+from concourse.masks import make_identity
 
 K, T, E, C, H, N = 1024, 1024, 4, 256, 512, 128
 FLOPS = 2 * E * C * (K * H + H * N)
@@ -22,9 +23,11 @@ PASSES = K // K_PASS
 HALF = C // 2
 LIST_COLS = C // 16
 
-VECTOR_SHARE = 44
-LEAD = 240
-LAST_SHARE = 42
+LEAD = C - 16
+FIRST = 40
+VECTOR_SHARE = 48
+LAST_SHARES = (32, 72)
+HALVED = ((0, 0), (E - 1, 1))
 
 
 def tile_moe_two_mlp_silu_kernel(
@@ -43,9 +46,8 @@ def tile_moe_two_mlp_silu_kernel(
         dst_sb = keep.tile([P, E * LIST_COLS], U16, name="dst_sb")
         tok_scales = sb("tok_scales", [P, T // 4], I32)
         tok_words = [sb("tok_words%d" % o, [P, T], I32) for o in range(PASSES)]
-        stage = [[sb("stage%d_%d" % (e, o), [P, LEAD + PACK * H // 2], F32) for o in range(PASSES)] for e in range(E)]
-        w1_low = [[stage[e][o][:, LEAD:].rearrange("p (j c) -> p j c", j=PACK) for o in range(PASSES)] for e in range(E)]
-        w1_high = [[sb("w1_high%d_%d" % (e, o), [P, PACK, H // 2], F32) for o in range(PASSES)] for e in range(E)]
+        stage = [[sb("stage%d_%d" % (e, o), [P, LEAD + PACK * H], F32) for o in range(PASSES)] for e in range(E)]
+        w1_raw = [[stage[e][o][:, LEAD:].rearrange("p (j c) -> p j c", j=PACK) for o in range(PASSES)] for e in range(E)]
         w1_bf = [[sb("w1_bf%d_%d" % (e, o), [P, PACK, P, PACK], BF16) for o in range(PASSES)] for e in range(E)]
         w1_codes = [[sb("w1_codes%d_%d" % (e, o), [P, H], U32) for o in range(PASSES)] for e in range(E)]
         w1_scales = [[sb("w1_scales%d_%d" % (e, o), [P, H], U8) for o in range(PASSES)] for e in range(E)]
@@ -53,39 +55,40 @@ def tile_moe_two_mlp_silu_kernel(
         w2_bf = [sb("w2_bf%d" % e, [P, N, PACK], BF16) for e in range(E)]
         w2_codes = [sb("w2_codes%d" % e, [P, N], U32) for e in range(E)]
         w2_scales = [sb("w2_scales%d" % e, [P, N], U8) for e in range(E)]
-        gate_sb = [sb("gate_sb%d" % e, [P, C], F32) for e in range(E)]
-        slot_words = [sb("slot_words%d" % o, [P, E * C], U32) for o in range(PASSES)]
-        slot_scales = sb("slot_scales", [P, E * C], U8)
-        h_bf = [
-            stage[e + 1][0][:, LEAD + 2 * C :].bitcast(BF16).rearrange("p (n t) -> p n t", t=PACK) for e in range(E - 1)
+        gate_col = sb("gate_col", [P, T // P], F32)
+        gate_sb = sb("gate_sb", [P, T], F32)
+        identity = sb("identity", [P, P], F32)
+        slot_words = [
+            [sb("slot_words%d_%d" % (g, o), [P, 2 * C], U32, "w1_bf0_1" if g and o else "") for o in range(PASSES)] for g in range(E // 2)
         ]
-        h_bf[0] = w1_high[1][0][:, 0:2, :].rearrange("p j c -> p (j c)").bitcast(BF16).rearrange("p (n t) -> p n t", t=PACK)
+        slot_scales = [sb("slot_scales%d" % g, [P, 2 * C], U8) for g in range(E // 2)]
+        h_bf = [stage[e + 1][0][:, 0 : 2 * C].bitcast(BF16).rearrange("p (n t) -> p n t", t=PACK) for e in range(E - 1)]
         h_bf.append(sb("h_bf", [P, C, PACK], BF16))
         h_codes = [sb("h_codes%d" % e, [P, C], U32) for e in range(E)]
         h_scales = [sb("h_scales%d" % e, [P, C], U8) for e in range(E)]
-        y_sb = [stage[e + 2][0][:, 0:C] for e in range(E - 2)]
-        y_sb.append(w1_high[E - 1][1][:, 0, :])
+        y_sb = [stage[e + 1][1][:, 0:C] for e in range(E - 2)]
+        y_sb.append(w1_raw[E - 1][1][:, 2, 0:C])
         y_sb.append(sb("y_sb", [P, C], F32))
         out_sb = sb("out_sb", [P, T], F32)
         warm_in = sb("warm_in", [P, 16], F32)
         warm_out = sb("warm_out", [P, 16], F32)
 
-        def load_w1_half(e, o, s):
-            rows = w1[e, o * K_PASS : (o + 1) * K_PASS, s * H // 2 : (s + 1) * H // 2]
-            nc.sync.dma_start(out=(w1_low, w1_high)[s][e][o][:], in_=rows.rearrange("(p j) c -> p j c", j=PACK))
+        def load_w1_rows(e, o, j0, j1):
+            rows = w1[e, o * K_PASS : (o + 1) * K_PASS, :].rearrange("(p j) c -> p j c", j=PACK)
+            nc.sync.dma_start(out=w1_raw[e][o][:, j0:j1, :], in_=rows[:, j0:j1, :])
 
         def load_w1(e, o):
-            load_w1_half(e, o, 0)
-            load_w1_half(e, o, 1)
+            if (e, o) in HALVED:
+                load_w1_rows(e, o, 0, 2)
+                load_w1_rows(e, o, 2, PACK)
+            else:
+                load_w1_rows(e, o, 0, PACK)
 
         def load_words(o):
             nc.sync.dma_start(out=tok_words[o][:], in_=x_words[o].rearrange("p t r -> p (t r)").bitcast(I32))
 
         def load_w2(e):
             nc.sync.dma_start(out=w2_raw[e][:], in_=w2[e].rearrange("(p j) n -> p j n", j=PACK))
-
-        def load_gate(e):
-            nc.sync.dma_start(out=gate_sb[e][:], in_=gate[:, e * C : (e + 1) * C])
 
         def load_scales():
             for q in range(4):
@@ -94,33 +97,40 @@ def tile_moe_two_mlp_silu_kernel(
                     in_=x_scales[:, 4 * q : 4 * q + 4, :].bitcast(I32),
                 )
 
-        def gather_scales(e0, e1):
-            entries = offs_sb[:, e0 * LIST_COLS : e1 * LIST_COLS]
-            nc.vector.tensor_copy(slot_scales[:, e0 * C : e1 * C], tok_scales[:].bitcast(U8).indirect(entries))
+        def spread_gate():
+            by_column = gate_sb[:].rearrange("p (s c) -> p s c", s=P)
+            for c0 in range(0, T // P, PACK):
+                spread = psum_y.tile([P, PACK, P], F32, name="y_ps")
+                for c in range(PACK):
+                    nc.tensor.transpose(spread[:, c, :], gate_col[:, c0 + c : c0 + c + 1].to_broadcast([P, P]), identity[:])
+                nc.scalar.copy(by_column[:, :, c0 : c0 + PACK], spread[:].rearrange("p c s -> p s c"))
 
-        def gather_words(o, e0, e1):
-            entries = offs_sb[:, e0 * LIST_COLS : e1 * LIST_COLS]
-            nc.vector.tensor_copy(slot_words[o][:, e0 * C : e1 * C], tok_words[o][:].bitcast(U32).indirect(entries))
+        def pair_list(g):
+            return offs_sb[:, 2 * g * LIST_COLS : 2 * (g + 1) * LIST_COLS]
 
-        def cast_w1(copy, e, o, m0, m1):
-            raw, base = (w1_low[e][o], 0) if m0 < P // 2 else (w1_high[e][o], P // 2)
+        def gather_scales(g):
+            nc.vector.tensor_copy(slot_scales[g][:], tok_scales[:].bitcast(U8).indirect(pair_list(g)))
+
+        def gather_words(g, o):
+            nc.vector.tensor_copy(slot_words[g][o][:], tok_words[o][:].bitcast(U32).indirect(pair_list(g)))
+
+        def cast_w1(copy, e, o, m0, m1, j0, j1):
             copy(
-                w1_bf[e][o][:, :, m0:m1, :].rearrange("p t m j -> p m j t"),
-                raw[:, :, PACK * (m0 - base) : PACK * (m1 - base)].rearrange("p j (m t) -> p m j t", t=PACK),
+                w1_bf[e][o][:, :, m0:m1, j0:j1].rearrange("p t m j -> p m j t"),
+                w1_raw[e][o][:, j0:j1, PACK * m0 : PACK * m1].rearrange("p j (m t) -> p m j t", t=PACK),
             )
 
-        def cast_high(e, o, share):
-            cast_w1(nc.scalar.copy, e, o, P // 2, P - share)
-            if share:
-                cast_w1(nc.vector.tensor_copy, e, o, P - share, P)
-
         def cast_block(e, o, share):
-            if o == 0 and e > 1:
-                cast_w1(nc.scalar.copy, e, o, 0, P // 4)
-                cast_w1(nc.scalar.copy, e, o, P // 4, P // 2)
-            else:
-                cast_w1(nc.scalar.copy, e, o, 0, P // 2)
-            cast_high(e, o, share)
+            cast_w1(nc.scalar.copy, e, o, 0, FIRST, 0, PACK)
+            cast_w1(nc.scalar.copy, e, o, FIRST, P - share, 0, PACK)
+            if share:
+                cast_w1(nc.vector.tensor_copy, e, o, P - share, P, 0, PACK)
+
+        def cast_halves(e, o, shares):
+            for j0, share in zip((0, 2), shares):
+                cast_w1(nc.scalar.copy, e, o, 0, P - share, j0, j0 + 2)
+                if share:
+                    cast_w1(nc.vector.tensor_copy, e, o, P - share, P, j0, j0 + 2)
 
         def quantise_w1(e, o, t0, t1):
             nc.vector.quantize_mx(
@@ -144,18 +154,18 @@ def tile_moe_two_mlp_silu_kernel(
 
         banks = {}
 
-        def first_layer(e, o, ts):
+        def first_layer(e, o):
             for half in range(2):
-                cols = slice(e * C + half * HALF, e * C + (half + 1) * HALF)
-                if (e, half) not in banks:
+                cols = slice((e % 2) * C + half * HALF, (e % 2) * C + (half + 1) * HALF)
+                if o == 0:
                     banks[(e, half)] = psum_a.tile([P, PACK, HALF], F32, name="bank")
-                for t in ts:
+                for t in range(PACK):
                     nc.tensor.matmul_mx(
                         out=banks[(e, half)][:, t, :],
                         lhsT=w1_codes[e][o][:, t * P : (t + 1) * P].bitcast(FP8X4),
                         lhsT_scale=w1_scales[e][o][:, t * P : (t + 1) * P],
-                        rhs=slot_words[o][:, cols].bitcast(FP8X4),
-                        rhs_scale=slot_scales[4 * o : P, cols],
+                        rhs=slot_words[e // 2][o][:, cols].bitcast(FP8X4),
+                        rhs_scale=slot_scales[e // 2][4 * o : P, cols],
                         start=(o == 0 and t == 0),
                         stop=(o == PASSES - 1 and t == PACK - 1),
                     )
@@ -186,58 +196,62 @@ def tile_moe_two_mlp_silu_kernel(
         def scatter(e, c0, c1, y_ps):
             nc.scalar.copy(y_sb[e][:, c0:c1], y_ps[:])
             places = dst_sb[:, (e * C + c0) // 16 : (e * C + c1) // 16]
-            nc.vector.tensor_tensor(out_sb[:].indirect(places), y_sb[e][:, c0:c1], gate_sb[e][:, c0:c1], MULT)
+            nc.vector.tensor_tensor(out_sb[:].indirect(places), y_sb[e][:, c0:c1], gate_sb[:, e * C + c0 : e * C + c1], MULT)
 
-        nc.gpsimd.memset(tok_scales[:], 0)
+        nc.vector.memset(tok_scales[:], 0)
         nc.gpsimd.memset(warm_in[:], 0.0)
+        make_identity(nc, identity[:])
         nc.scalar.activation(warm_out[:], warm_in[:], SILU)
         nc.sync.dma_start(offs_sb[:], offs)
-        load_w1_half(0, 0, 0)
+        nc.sync.dma_start(out=gate_col[:], in_=gate[0].rearrange("(p c) -> p c", p=P))
+        load_w1_rows(0, 0, 0, 2)
         load_scales()
-        load_w1_half(0, 0, 1)
-        load_w1_half(0, 1, 0)
         load_words(0)
-        load_w1_half(0, 1, 1)
+        load_w1_rows(0, 0, 2, PACK)
+        load_w1(0, 1)
+        load_words(1)
         for e in range(1, E):
-            load_w1_half(e, 0, 0)
-            if e == 1:
-                load_words(1)
-            load_w1_half(e, 0, 1)
+            load_w1(e, 0)
             load_w2(e - 1)
             if e == 1:
                 nc.sync.dma_start(dst_sb[:], dst)
-            else:
-                load_gate(e - 2)
             load_w1(e, 1)
         load_w2(E - 1)
-        load_gate(E - 2)
-        load_gate(E - 1)
 
-        gather_scales(0, 1)
-        gather_scales(1, E)
-        for o in range(PASSES):
-            cast_block(0, o, 0)
-            gather_words(o, 0, 1)
-            quantise_w1(0, o, 0, PACK)
-            first_layer(0, o, range(PACK))
-            gather_words(o, 1, E)
-        y_ps = None
+        spread_gate()
+        gather_scales(0)
+        gather_scales(1)
+        cast_halves(0, 0, (0, 0))
+        gather_words(0, 0)
+        gather_words(1, 0)
+        quantise_w1(0, 0, 0, PACK)
+        first_layer(0, 0)
+        cast_block(0, 1, 0)
+        gather_words(0, 1)
+        quantise_w1(0, 1, 0, PACK)
+        first_layer(0, 1)
+        gather_words(1, 1)
         for e in range(1, E):
-            last = e == E - 1
-            cast_w2(nc.vector.tensor_copy, e - 1)
-            cast_block(e, 0, VECTOR_SHARE if e > 1 else 0)
-            quantise_w2(e - 1)
-            quantise_w1(e, 0, 0, PACK)
-            first_layer(e, 0, range(PACK))
-            if e > 1:
-                scatter(e - 2, 0, C, y_ps)
+            share = VECTOR_SHARE
+            cast_w1(nc.scalar.copy, e, 0, 0, 34, 0, PACK)
+            cast_w1(nc.scalar.copy, e, 0, 34, 68, 0, PACK)
             silu(e - 1)
-            cast_block(e, 1, LAST_SHARE if last else VECTOR_SHARE)
+            cast_w1(nc.scalar.copy, e, 0, 68, P - share, 0, PACK)
+            if share:
+                cast_w1(nc.vector.tensor_copy, e, 0, P - share, P, 0, PACK)
+            cast_w2(nc.vector.tensor_copy, e - 1)
+            quantise_w2(e - 1)
             y_ps = second_layer(e - 1, 0, C)
+            quantise_w1(e, 0, 0, PACK)
+            first_layer(e, 0)
+            if e < E - 1:
+                cast_block(e, 1, VECTOR_SHARE)
+            else:
+                cast_halves(e, 1, LAST_SHARES)
             quantise_w1(e, 1, 0, 2)
             quantise_w1(e, 1, 2, PACK)
-            first_layer(e, 1, range(PACK))
-        scatter(E - 2, 0, C, y_ps)
+            first_layer(e, 1)
+            scatter(e - 1, 0, C, y_ps)
         cast_w2(nc.scalar.copy, E - 1)
         quantise_w2(E - 1)
         silu(E - 1)

@@ -26,8 +26,8 @@ LIST_COLS = C // 16
 LEAD = C - 16
 FIRST = 40
 VECTOR_SHARE = 48
-LAST_SHARES = (32, 72)
-HALVED = ((0, 0), (E - 1, 1))
+LAST_SHARES = (0, 48)
+HALVED = ((E - 1, 1),)
 
 
 def tile_moe_two_mlp_silu_kernel(
@@ -67,22 +67,22 @@ def tile_moe_two_mlp_silu_kernel(
         h_codes = [sb("h_codes%d" % e, [P, C], U32) for e in range(E)]
         h_scales = [sb("h_scales%d" % e, [P, C], U8) for e in range(E)]
         y_sb = [stage[e + 1][1][:, 0:C] for e in range(E - 2)]
-        y_sb.append(w1_raw[E - 1][1][:, 2, 0:C])
+        y_sb.append(w1_raw[E - 1][1][:, 2, C:H])
         y_sb.append(sb("y_sb", [P, C], F32))
         out_sb = sb("out_sb", [P, T], F32)
         warm_in = sb("warm_in", [P, 16], F32)
         warm_out = sb("warm_out", [P, 16], F32)
 
-        def load_w1_rows(e, o, j0, j1):
-            rows = w1[e, o * K_PASS : (o + 1) * K_PASS, :].rearrange("(p j) c -> p j c", j=PACK)
-            nc.sync.dma_start(out=w1_raw[e][o][:, j0:j1, :], in_=rows[:, j0:j1, :])
+        def load_w1_columns(e, o, c0, c1):
+            rows = w1[e, o * K_PASS : (o + 1) * K_PASS, c0:c1].rearrange("(p j) c -> p j c", j=PACK)
+            nc.sync.dma_start(out=w1_raw[e][o][:, :, c0:c1], in_=rows)
 
         def load_w1(e, o):
             if (e, o) in HALVED:
-                load_w1_rows(e, o, 0, 2)
-                load_w1_rows(e, o, 2, PACK)
+                load_w1_columns(e, o, 0, H // 2)
+                load_w1_columns(e, o, H // 2, H)
             else:
-                load_w1_rows(e, o, 0, PACK)
+                load_w1_columns(e, o, 0, H)
 
         def load_words(o):
             nc.sync.dma_start(out=tok_words[o][:], in_=x_words[o].rearrange("p t r -> p (t r)").bitcast(I32))
@@ -127,10 +127,10 @@ def tile_moe_two_mlp_silu_kernel(
                 cast_w1(nc.vector.tensor_copy, e, o, P - share, P, 0, PACK)
 
         def cast_halves(e, o, shares):
-            for j0, share in zip((0, 2), shares):
-                cast_w1(nc.scalar.copy, e, o, 0, P - share, j0, j0 + 2)
+            for m0, share in zip((0, P // 2), shares):
+                cast_w1(nc.scalar.copy, e, o, m0, m0 + P // 2 - share, 0, PACK)
                 if share:
-                    cast_w1(nc.vector.tensor_copy, e, o, P - share, P, j0, j0 + 2)
+                    cast_w1(nc.vector.tensor_copy, e, o, m0 + P // 2 - share, m0 + P // 2, 0, PACK)
 
         def quantise_w1(e, o, t0, t1):
             nc.vector.quantize_mx(
@@ -204,10 +204,9 @@ def tile_moe_two_mlp_silu_kernel(
         nc.scalar.activation(warm_out[:], warm_in[:], SILU)
         nc.sync.dma_start(offs_sb[:], offs)
         nc.sync.dma_start(out=gate_col[:], in_=gate[0].rearrange("(p c) -> p c", p=P))
-        load_w1_rows(0, 0, 0, 2)
-        load_scales()
         load_words(0)
-        load_w1_rows(0, 0, 2, PACK)
+        load_scales()
+        load_w1(0, 0)
         load_w1(0, 1)
         load_words(1)
         for e in range(1, E):
@@ -221,7 +220,7 @@ def tile_moe_two_mlp_silu_kernel(
         spread_gate()
         gather_scales(0)
         gather_scales(1)
-        cast_halves(0, 0, (0, 0))
+        cast_block(0, 0, 0)
         gather_words(0, 0)
         gather_words(1, 0)
         quantise_w1(0, 0, 0, PACK)

@@ -1,7 +1,6 @@
 from contextlib import ExitStack
 
 import concourse.mybir as mybir
-from concourse.masks import make_identity
 
 K, T, E, C, H, N = 1024, 1024, 4, 256, 512, 128
 FLOPS = 2 * E * C * (K * H + H * N)
@@ -55,9 +54,7 @@ def tile_moe_two_mlp_silu_kernel(
         w2_bf = [sb("w2_bf%d" % e, [P, N, PACK], BF16) for e in range(E)]
         w2_codes = [sb("w2_codes%d" % e, [P, N], U32) for e in range(E)]
         w2_scales = [sb("w2_scales%d" % e, [P, N], U8) for e in range(E)]
-        gate_col = sb("gate_col", [P, T // P], F32)
         gate_sb = sb("gate_sb", [P, T], F32)
-        identity = sb("identity", [P, P], F32)
         slot_words = [
             [sb("slot_words%d_%d" % (g, o), [P, 2 * C], U32, "w1_bf0_1" if g and o else "") for o in range(PASSES)] for g in range(E // 2)
         ]
@@ -97,13 +94,8 @@ def tile_moe_two_mlp_silu_kernel(
                     in_=x_scales[:, 4 * q : 4 * q + 4, :].bitcast(I32),
                 )
 
-        def spread_gate():
-            by_column = gate_sb[:].rearrange("p (s c) -> p s c", s=P)
-            for c0 in range(0, T // P, PACK):
-                spread = psum_y.tile([P, PACK, P], F32, name="y_ps")
-                for c in range(PACK):
-                    nc.tensor.transpose(spread[:, c, :], gate_col[:, c0 + c : c0 + c + 1].to_broadcast([P, P]), identity[:])
-                nc.scalar.copy(by_column[:, :, c0 : c0 + PACK], spread[:].rearrange("p c s -> p s c"))
+        def load_gate(c0, c1):
+            nc.sync.dma_start(out=gate_sb[:, c0:c1], in_=gate[:, c0:c1])
 
         def pair_list(g):
             return offs_sb[:, 2 * g * LIST_COLS : 2 * (g + 1) * LIST_COLS]
@@ -200,10 +192,8 @@ def tile_moe_two_mlp_silu_kernel(
 
         nc.vector.memset(tok_scales[:], 0)
         nc.gpsimd.memset(warm_in[:], 0.0)
-        make_identity(nc, identity[:])
         nc.scalar.activation(warm_out[:], warm_in[:], SILU)
         nc.sync.dma_start(offs_sb[:], offs)
-        nc.sync.dma_start(out=gate_col[:], in_=gate[0].rearrange("(p c) -> p c", p=P))
         load_words(0)
         load_scales()
         load_w1(0, 0)
@@ -211,13 +201,15 @@ def tile_moe_two_mlp_silu_kernel(
         load_words(1)
         for e in range(1, E):
             load_w1(e, 0)
+            if e == 1:
+                load_gate(0, 2 * C)
             load_w2(e - 1)
             if e == 1:
                 nc.sync.dma_start(dst_sb[:], dst)
             load_w1(e, 1)
         load_w2(E - 1)
+        load_gate(2 * C, E * C)
 
-        spread_gate()
         gather_scales(0)
         gather_scales(1)
         cast_block(0, 0, 0)

@@ -14,6 +14,8 @@ U8 = mybir.dt.uint8
 FP8X4 = mybir.dt.float8_e4m3fn_x4
 SILU = mybir.ActivationFunctionType.Silu
 MULT = mybir.AluOpType.mult
+ADD = mybir.AluOpType.add
+EQUAL = mybir.AluOpType.is_equal
 
 P = 128
 PACK = 4
@@ -22,11 +24,12 @@ PASSES = K // K_PASS
 HALF = C // 2
 LIST_COLS = C // 16
 
-LEAD = C - 16
+LEAD = C
+OVERLAP = 16
 FIRST = 40
-VECTOR_SHARE = 48
-LAST_SHARES = (0, 48)
-HALVED = ((E - 1, 1),)
+VECTOR_SHARE = 56
+LAST_SHARES = (0,0)
+HALVED = ()
 
 
 def tile_moe_two_mlp_silu_kernel(
@@ -38,14 +41,14 @@ def tile_moe_two_mlp_silu_kernel(
         psum_a = ctx.enter_context(tc.psum_pool(name="psum_a", bufs=6))
         psum_y = ctx.enter_context(tc.psum_pool(name="psum_y", bufs=2))
 
-        def sb(name, shape, dtype, tag=""):
-            return keep.tile(shape, dtype, name=name, tag=tag or name, align_bytes=64)
+        def sb(name, shape, dtype, tag="", align=64):
+            return keep.tile(shape, dtype, name=name, tag=tag or name, align_bytes=align)
 
         offs_sb = keep.tile([P, E * LIST_COLS], U16, name="offs_sb")
         dst_sb = keep.tile([P, E * LIST_COLS], U16, name="dst_sb")
         tok_scales = sb("tok_scales", [P, T // 4], I32)
         tok_words = [sb("tok_words%d" % o, [P, T], I32) for o in range(PASSES)]
-        stage = [[sb("stage%d_%d" % (e, o), [P, LEAD + PACK * H], F32) for o in range(PASSES)] for e in range(E)]
+        stage = [[sb("stage%d_%d" % (e, o), [P, LEAD + PACK * H], F32, "", 256) for o in range(PASSES)] for e in range(E)]
         w1_raw = [[stage[e][o][:, LEAD:].rearrange("p (j c) -> p j c", j=PACK) for o in range(PASSES)] for e in range(E)]
         w1_bf = [[sb("w1_bf%d_%d" % (e, o), [P, PACK, P, PACK], BF16) for o in range(PASSES)] for e in range(E)]
         w1_codes = [[sb("w1_codes%d_%d" % (e, o), [P, H], U32) for o in range(PASSES)] for e in range(E)]
@@ -54,16 +57,21 @@ def tile_moe_two_mlp_silu_kernel(
         w2_bf = [sb("w2_bf%d" % e, [P, N, PACK], BF16) for e in range(E)]
         w2_codes = [sb("w2_codes%d" % e, [P, N], U32) for e in range(E)]
         w2_scales = [sb("w2_scales%d" % e, [P, N], U8) for e in range(E)]
+        gate_col = sb("gate_col", [P, T // P], F32)
         gate_sb = sb("gate_sb", [P, T], F32)
+        identity = sb("identity", [P, P], F32)
+        ones = sb("ones", [P, 32], F32)
+        column = sb("column", [P, 32], F32)
+        row = sb("row", [P, 32], F32)
         slot_words = [
             [sb("slot_words%d_%d" % (g, o), [P, 2 * C], U32, "w1_bf0_1" if g and o else "") for o in range(PASSES)] for g in range(E // 2)
         ]
         slot_scales = [sb("slot_scales%d" % g, [P, 2 * C], U8) for g in range(E // 2)]
-        h_bf = [stage[e + 1][0][:, 0 : 2 * C].bitcast(BF16).rearrange("p (n t) -> p n t", t=PACK) for e in range(E - 1)]
+        h_bf = [stage[e + 1][0][:, OVERLAP : OVERLAP + 2 * C].bitcast(BF16).rearrange("p (n t) -> p n t", t=PACK) for e in range(E - 1)]
         h_bf.append(sb("h_bf", [P, C, PACK], BF16))
         h_codes = [sb("h_codes%d" % e, [P, C], U32) for e in range(E)]
         h_scales = [sb("h_scales%d" % e, [P, C], U8) for e in range(E)]
-        y_sb = [stage[e + 1][1][:, 0:C] for e in range(E - 2)]
+        y_sb = [stage[e + 1][1][:, OVERLAP : OVERLAP + C] for e in range(E - 2)]
         y_sb.append(w1_raw[E - 1][1][:, 2, C:H])
         y_sb.append(sb("y_sb", [P, C], F32))
         out_sb = sb("out_sb", [P, T], F32)
@@ -94,8 +102,21 @@ def tile_moe_two_mlp_silu_kernel(
                     in_=x_scales[:, 4 * q : 4 * q + 4, :].bitcast(I32),
                 )
 
-        def load_gate(c0, c1):
-            nc.sync.dma_start(out=gate_sb[:, c0:c1], in_=gate[:, c0:c1])
+        def build_identity():
+            nc.vector.memset(ones[:], 1.0)
+            nc.vector.memset(identity[:], 0.0)
+            nc.vector.tensor_tensor_scan(column[:], ones[:], ones[:], 0.0, MULT, ADD)
+            nc.vector.transpose(row[:], column[:])
+            for q in range(0, P, 32):
+                nc.vector.tensor_tensor(identity[q : q + 32, q : q + 32], row[q : q + 32, :], column[q : q + 32, :], EQUAL)
+
+        def spread_gate():
+            by_column = gate_sb[:].rearrange("p (s c) -> p s c", s=P)
+            for c0 in range(0, T // P, PACK):
+                spread = psum_y.tile([P, PACK, P], F32, name="y_ps")
+                for c in range(PACK):
+                    nc.tensor.transpose(spread[:, c, :], gate_col[:, c0 + c : c0 + c + 1].to_broadcast([P, P]), identity[:])
+                nc.scalar.copy(by_column[:, :, c0 : c0 + PACK], spread[:].rearrange("p c s -> p s c"))
 
         def pair_list(g):
             return offs_sb[:, 2 * g * LIST_COLS : 2 * (g + 1) * LIST_COLS]
@@ -192,32 +213,32 @@ def tile_moe_two_mlp_silu_kernel(
 
         nc.vector.memset(tok_scales[:], 0)
         nc.gpsimd.memset(warm_in[:], 0.0)
+        build_identity()
         nc.scalar.activation(warm_out[:], warm_in[:], SILU)
-        nc.sync.dma_start(offs_sb[:], offs)
         load_words(0)
+        nc.sync.dma_start(offs_sb[:], offs)
+        nc.sync.dma_start(out=gate_col[:], in_=gate[0].rearrange("(p c) -> p c", p=P))
         load_scales()
         load_w1(0, 0)
         load_w1(0, 1)
         load_words(1)
         for e in range(1, E):
             load_w1(e, 0)
-            if e == 1:
-                load_gate(0, 2 * C)
             load_w2(e - 1)
             if e == 1:
                 nc.sync.dma_start(dst_sb[:], dst)
             load_w1(e, 1)
         load_w2(E - 1)
-        load_gate(2 * C, E * C)
 
+        spread_gate()
         gather_scales(0)
         gather_scales(1)
-        cast_block(0, 0, 0)
+        cast_w1(nc.scalar.copy, 0, 0, 0, P, 0, PACK)
         gather_words(0, 0)
         gather_words(1, 0)
         quantise_w1(0, 0, 0, PACK)
         first_layer(0, 0)
-        cast_block(0, 1, 0)
+        cast_w1(nc.scalar.copy, 0, 1, 0, P, 0, PACK)
         gather_words(0, 1)
         quantise_w1(0, 1, 0, PACK)
         first_layer(0, 1)
@@ -236,9 +257,9 @@ def tile_moe_two_mlp_silu_kernel(
             quantise_w1(e, 0, 0, PACK)
             first_layer(e, 0)
             if e < E - 1:
-                cast_block(e, 1, VECTOR_SHARE)
+                cast_block(e, 1, 56)
             else:
-                cast_halves(e, 1, LAST_SHARES)
+                cast_block(e, 1, 64)
             quantise_w1(e, 1, 0, 2)
             quantise_w1(e, 1, 2, PACK)
             first_layer(e, 1)

@@ -93,7 +93,9 @@ def tile_moe_two_mlp_silu_kernel(
             nc.sync.dma_start(out=tok_words[o][:], in_=x_words[o].rearrange("p t r -> p (t r)").bitcast(I32))
 
         def load_w2(e):
-            nc.sync.dma_start(out=w2_raw[e][:], in_=w2[e].rearrange("(p j) n -> p j n", j=PACK))
+            rows = w2[e].rearrange("(g t u) n -> u g t n", t=PACK, u=2)
+            for u in range(2):
+                nc.sync.dma_start(out=w2_raw[e][u:P:2], in_=rows[u])
 
         def load_scales():
             for q in range(4):
@@ -129,8 +131,8 @@ def tile_moe_two_mlp_silu_kernel(
 
         def cast_w1(copy, e, o, m0, m1, j0, j1):
             copy(
-                w1_bf[e][o][:, :, m0:m1, j0:j1].rearrange("p t m j -> p m j t"),
-                w1_raw[e][o][:, j0:j1, PACK * m0 : PACK * m1].rearrange("p j (m t) -> p m j t", t=PACK),
+                w1_bf[e][o][:, :, m0:m1, j0:j1].rearrange("p t (g u) j -> p g t j u", u=2),
+                w1_raw[e][o][:, j0:j1, PACK * m0 : PACK * m1].rearrange("p j (g t u) -> p g t j u", t=PACK, u=2),
             )
 
         def cast_block(e, o, share):

@@ -23,13 +23,15 @@ K_PASS = P * PACK
 PASSES = K // K_PASS
 HALF = C // 2
 LIST_COLS = C // 16
+QUADRANT = 32
 
 LEAD = C
 OVERLAP = 16
-FIRST = 40
+UNDER_H = (C + OVERLAP) // PACK
+
 VECTOR_SHARE = 56
-LAST_SHARES = (0,0)
-HALVED = ()
+LAST_SHARE = 64
+FIRST_PART = 40
 
 
 def tile_moe_two_mlp_silu_kernel(
@@ -60,9 +62,9 @@ def tile_moe_two_mlp_silu_kernel(
         gate_col = sb("gate_col", [P, T // P], F32)
         gate_sb = sb("gate_sb", [P, T], F32)
         identity = sb("identity", [P, P], F32)
-        ones = sb("ones", [P, 32], F32)
-        column = sb("column", [P, 32], F32)
-        row = sb("row", [P, 32], F32)
+        ones = sb("ones", [P, QUADRANT], F32)
+        column = sb("column", [P, QUADRANT], F32)
+        row = sb("row", [P, QUADRANT], F32)
         slot_words = [
             [sb("slot_words%d_%d" % (g, o), [P, 2 * C], U32, "w1_bf0_1" if g and o else "") for o in range(PASSES)] for g in range(E // 2)
         ]
@@ -78,29 +80,22 @@ def tile_moe_two_mlp_silu_kernel(
         warm_in = sb("warm_in", [P, 16], F32)
         warm_out = sb("warm_out", [P, 16], F32)
 
-        def load_w1_columns(e, o, c0, c1):
-            rows = w1[e, o * K_PASS : (o + 1) * K_PASS, c0:c1].rearrange("(p j) c -> p j c", j=PACK)
-            nc.sync.dma_start(out=w1_raw[e][o][:, :, c0:c1], in_=rows)
-
         def load_w1(e, o):
-            if (e, o) in HALVED:
-                load_w1_columns(e, o, 0, H // 2)
-                load_w1_columns(e, o, H // 2, H)
-            else:
-                load_w1_columns(e, o, 0, H)
+            rows = w1[e, o * K_PASS : (o + 1) * K_PASS, :].rearrange("(p j) c -> p j c", j=PACK)
+            nc.sync.dma_start(out=w1_raw[e][o], in_=rows)
 
         def load_words(o):
             nc.sync.dma_start(out=tok_words[o][:], in_=x_words[o].rearrange("p t r -> p (t r)").bitcast(I32))
 
         def load_w2(e):
-            rows = w2[e].rearrange("(g t u) n -> u g t n", t=PACK, u=2)
-            for u in range(2):
-                nc.sync.dma_start(out=w2_raw[e][u:P:2], in_=rows[u])
+            rows = w2[e].rearrange("(g a u b) n -> a g u (b n)", a=2, u=2, b=2)
+            for a in range(2):
+                nc.sync.dma_start(out=w2_raw[e][:, 2 * a : 2 * a + 2, :].rearrange("p b n -> p (b n)"), in_=rows[a])
 
         def load_scales():
-            for q in range(4):
+            for q in range(P // QUADRANT):
                 nc.sync.dma_start(
-                    out=tok_scales[32 * q : 32 * q + 4 * PASSES, :],
+                    out=tok_scales[QUADRANT * q : QUADRANT * q + 4 * PASSES, :],
                     in_=x_scales[:, 4 * q : 4 * q + 4, :].bitcast(I32),
                 )
 
@@ -109,8 +104,9 @@ def tile_moe_two_mlp_silu_kernel(
             nc.vector.memset(identity[:], 0.0)
             nc.vector.tensor_tensor_scan(column[:], ones[:], ones[:], 0.0, MULT, ADD)
             nc.vector.transpose(row[:], column[:])
-            for q in range(0, P, 32):
-                nc.vector.tensor_tensor(identity[q : q + 32, q : q + 32], row[q : q + 32, :], column[q : q + 32, :], EQUAL)
+            for p0 in range(0, P, QUADRANT):
+                part = slice(p0, p0 + QUADRANT)
+                nc.vector.tensor_tensor(identity[part, part], row[part, :], column[part, :], EQUAL)
 
         def spread_gate():
             by_column = gate_sb[:].rearrange("p (s c) -> p s c", s=P)
@@ -129,23 +125,11 @@ def tile_moe_two_mlp_silu_kernel(
         def gather_words(g, o):
             nc.vector.tensor_copy(slot_words[g][o][:], tok_words[o][:].bitcast(U32).indirect(pair_list(g)))
 
-        def cast_w1(copy, e, o, m0, m1, j0, j1):
+        def cast_w1(copy, e, o, m0, m1, t0, t1):
             copy(
-                w1_bf[e][o][:, :, m0:m1, j0:j1].rearrange("p t (g u) j -> p g t j u", u=2),
-                w1_raw[e][o][:, j0:j1, PACK * m0 : PACK * m1].rearrange("p j (g t u) -> p g t j u", t=PACK, u=2),
+                w1_bf[e][o][:, t0:t1, m0:m1, :].rearrange("p (a b) (g u) j -> p g a b j u", b=2, u=2),
+                w1_raw[e][o][:, :, PACK * m0 : PACK * m1].rearrange("p j (g a u b) -> p g a b j u", a=2, u=2, b=2)[:, :, t0 // 2 : t1 // 2],
             )
-
-        def cast_block(e, o, share):
-            cast_w1(nc.scalar.copy, e, o, 0, FIRST, 0, PACK)
-            cast_w1(nc.scalar.copy, e, o, FIRST, P - share, 0, PACK)
-            if share:
-                cast_w1(nc.vector.tensor_copy, e, o, P - share, P, 0, PACK)
-
-        def cast_halves(e, o, shares):
-            for m0, share in zip((0, P // 2), shares):
-                cast_w1(nc.scalar.copy, e, o, m0, m0 + P // 2 - share, 0, PACK)
-                if share:
-                    cast_w1(nc.vector.tensor_copy, e, o, m0 + P // 2 - share, m0 + P // 2, 0, PACK)
 
         def quantise_w1(e, o, t0, t1):
             nc.vector.quantize_mx(
@@ -217,6 +201,7 @@ def tile_moe_two_mlp_silu_kernel(
         nc.gpsimd.memset(warm_in[:], 0.0)
         build_identity()
         nc.scalar.activation(warm_out[:], warm_in[:], SILU)
+
         load_words(0)
         nc.sync.dma_start(offs_sb[:], offs)
         nc.sync.dma_start(out=gate_col[:], in_=gate[0].rearrange("(p c) -> p c", p=P))
@@ -246,26 +231,29 @@ def tile_moe_two_mlp_silu_kernel(
         first_layer(0, 1)
         gather_words(1, 1)
         for e in range(1, E):
-            share = VECTOR_SHARE
-            cast_w1(nc.scalar.copy, e, 0, 0, 34, 0, PACK)
-            cast_w1(nc.scalar.copy, e, 0, 34, 68, 0, PACK)
+            scalar_end = P - VECTOR_SHARE
+            cast_w1(nc.scalar.copy, e, 0, 0, UNDER_H // 2, 0, PACK)
+            cast_w1(nc.scalar.copy, e, 0, UNDER_H // 2, UNDER_H, 0, PACK)
+            cast_w1(nc.scalar.copy, e, 0, UNDER_H, scalar_end, 0, 2)
             silu(e - 1)
-            cast_w1(nc.scalar.copy, e, 0, 68, P - share, 0, PACK)
-            if share:
-                cast_w1(nc.vector.tensor_copy, e, 0, P - share, P, 0, PACK)
+            cast_w1(nc.scalar.copy, e, 0, UNDER_H, scalar_end, 2, PACK)
+            cast_w1(nc.vector.tensor_copy, e, 0, scalar_end, P, 0, PACK)
             cast_w2(nc.vector.tensor_copy, e - 1)
             quantise_w2(e - 1)
+            quantise_w1(e, 0, 0, 2)
             y_ps = second_layer(e - 1, 0, C)
-            quantise_w1(e, 0, 0, PACK)
+            quantise_w1(e, 0, 2, PACK)
             first_layer(e, 0)
-            if e < E - 1:
-                cast_block(e, 1, 56)
-            else:
-                cast_block(e, 1, 64)
+
+            scalar_end = P - (VECTOR_SHARE if e < E - 1 else LAST_SHARE)
+            cast_w1(nc.scalar.copy, e, 1, 0, FIRST_PART, 0, PACK)
+            cast_w1(nc.scalar.copy, e, 1, FIRST_PART, scalar_end, 0, PACK)
+            cast_w1(nc.vector.tensor_copy, e, 1, scalar_end, P, 0, PACK)
             quantise_w1(e, 1, 0, 2)
             quantise_w1(e, 1, 2, PACK)
             first_layer(e, 1)
             scatter(e - 1, 0, C, y_ps)
+
         cast_w2(nc.scalar.copy, E - 1)
         quantise_w2(E - 1)
         silu(E - 1)

@@ -126,10 +126,11 @@ def tile_moe_two_mlp_silu_kernel(
             nc.vector.tensor_copy(slot_words[g][o][:], tok_words[o][:].bitcast(U32).indirect(pair_list(g)))
 
         def cast_w1(copy, e, o, m0, m1, t0, t1):
-            copy(
-                w1_bf[e][o][:, t0:t1, m0:m1, :].rearrange("p (a b) (g u) j -> p g a b j u", b=2, u=2),
-                w1_raw[e][o][:, :, PACK * m0 : PACK * m1].rearrange("p j (g a u b) -> p g a b j u", a=2, u=2, b=2)[:, :, t0 // 2 : t1 // 2],
-            )
+            for a in range(t0 // 2, t1 // 2):
+                copy(
+                    w1_bf[e][o][:, 2 * a : 2 * a + 2, m0:m1, :].rearrange("p b (g u) j -> p g j u b", u=2),
+                    w1_raw[e][o][:, :, PACK * m0 : PACK * m1].rearrange("p j (g a u b) -> p a g j u b", a=2, u=2, b=2)[:, a],
+                )
 
         def quantise_w1(e, o, t0, t1):
             nc.vector.quantize_mx(

@@ -77,7 +77,6 @@ def tile_moe_two_mlp_silu_kernel(
         y_sb.append(w1_raw[E - 1][1][:, 2, C:H])
         y_sb.append(sb("y_sb", [P, C], F32))
         out_sb = sb("out_sb", [P, T], F32)
-        warm_in = sb("warm_in", [P, 16], F32)
         warm_out = sb("warm_out", [P, 16], F32)
 
         def load_w1(e, o):
@@ -92,12 +91,9 @@ def tile_moe_two_mlp_silu_kernel(
             for a in range(2):
                 nc.sync.dma_start(out=w2_raw[e][:, 2 * a : 2 * a + 2, :].rearrange("p b n -> p (b n)"), in_=rows[a])
 
-        def load_scales():
-            for q in range(P // QUADRANT):
-                nc.sync.dma_start(
-                    out=tok_scales[QUADRANT * q : QUADRANT * q + 4 * PASSES, :],
-                    in_=x_scales[:, 4 * q : 4 * q + 4, :].bitcast(I32),
-                )
+        def load_scales(o):
+            for r in range(4):
+                nc.sync.dma_start(out=tok_scales[4 * o + r : P : QUADRANT, :], in_=x_scales[o, r:16:4, :].bitcast(I32))
 
         def build_identity():
             nc.vector.memset(ones[:], 1.0)
@@ -199,15 +195,15 @@ def tile_moe_two_mlp_silu_kernel(
             nc.vector.tensor_tensor(out_sb[:].indirect(places), y_sb[e][:, c0:c1], gate_sb[:, e * C + c0 : e * C + c1], MULT)
 
         nc.vector.memset(tok_scales[:], 0)
-        nc.gpsimd.memset(warm_in[:], 0.0)
         build_identity()
-        nc.scalar.activation(warm_out[:], warm_in[:], SILU)
+        nc.scalar.activation(warm_out[:], ones[:, 0:16], SILU)
 
         load_words(0)
         nc.sync.dma_start(offs_sb[:], offs)
         nc.sync.dma_start(out=gate_col[:], in_=gate[0].rearrange("(p c) -> p c", p=P))
-        load_scales()
+        load_scales(0)
         load_w1(0, 0)
+        load_scales(1)
         load_w1(0, 1)
         load_words(1)
         for e in range(1, E):

@@ -32,6 +32,9 @@ UNDER_H = (C + OVERLAP) // PACK
 VECTOR_SHARE = 56
 LAST_SHARE = 64
 FIRST_PART = 40
+SPLIT2 = 1
+H1ORD = 0
+SH00 = 0
 
 
 def tile_moe_two_mlp_silu_kernel(
@@ -50,10 +53,10 @@ def tile_moe_two_mlp_silu_kernel(
         dst_sb = keep.tile([P, E * LIST_COLS], U16, name="dst_sb")
         tok_scales = sb("tok_scales", [P, T // 4], I32)
         tok_words = [sb("tok_words%d" % o, [P, T], I32) for o in range(PASSES)]
-        stage = [[sb("stage%d_%d" % (e, o), [P, LEAD + PACK * H], F32, "", 256) for o in range(PASSES)] for e in range(E)]
-        w1_raw = [[stage[e][o][:, LEAD:].rearrange("p (j c) -> p j c", j=PACK) for o in range(PASSES)] for e in range(E)]
+        stage = [[sb("stage%d_%d" % (e, o), [P, LEAD + PACK * H + 8], F32, "", 256) for o in range(PASSES)] for e in range(E)]
+        w1_raw = [[stage[e][o][:, LEAD : LEAD + PACK * H].rearrange("p (j c) -> p j c", j=PACK) for o in range(PASSES)] for e in range(E)]
         w1_bf = [[sb("w1_bf%d_%d" % (e, o), [P, PACK, P, PACK], BF16) for o in range(PASSES)] for e in range(E)]
-        w1_codes = [[sb("w1_codes%d_%d" % (e, o), [P, H], U32) for o in range(PASSES)] for e in range(E)]
+        w1_codes = [[sb("w1_codes%d_%d" % (e, o), [P, H], U32, "tok_scales" if e + o == 0 else "") for o in range(PASSES)] for e in range(E)]
         w1_scales = [[sb("w1_scales%d_%d" % (e, o), [P, H], U8) for o in range(PASSES)] for e in range(E)]
         w2_raw = [sb("w2_raw%d" % e, [P, PACK, N], F32) for e in range(E)]
         w2_bf = [sb("w2_bf%d" % e, [P, N, PACK], BF16) for e in range(E)]
@@ -74,8 +77,9 @@ def tile_moe_two_mlp_silu_kernel(
         h_codes = [sb("h_codes%d" % e, [P, C], U32) for e in range(E)]
         h_scales = [sb("h_scales%d" % e, [P, C], U8) for e in range(E)]
         y_sb = [stage[e + 1][1][:, OVERLAP : OVERLAP + C] for e in range(E - 2)]
-        y_sb.append(w1_raw[E - 1][1][:, 2, C:H])
+        y_sb.append(stage[E - 1][1][:, LEAD + PACK * H + 8 - C : LEAD + PACK * H + 8])
         y_sb.append(sb("y_sb", [P, C], F32))
+        y_late = stage[E - 1][1][:, LEAD + PACK * H : LEAD + PACK * H + 8]
         out_sb = sb("out_sb", [P, T], F32)
         warm_out = sb("warm_out", [P, 16], F32)
 
@@ -155,21 +159,25 @@ def tile_moe_two_mlp_silu_kernel(
                 cols = slice((e % 2) * C + half * HALF, (e % 2) * C + (half + 1) * HALF)
                 if o == 0:
                     banks[(e, half)] = psum_a.tile([P, PACK, HALF], F32, name="bank")
-                for t in range(PACK):
+                ts = [2, 3, 0, 1] if (H1ORD and half and o and e == E - 1) else [0, 1, 2, 3]
+                for t in ts:
                     nc.tensor.matmul_mx(
                         out=banks[(e, half)][:, t, :],
                         lhsT=w1_codes[e][o][:, t * P : (t + 1) * P].bitcast(FP8X4),
                         lhsT_scale=w1_scales[e][o][:, t * P : (t + 1) * P],
                         rhs=slot_words[e // 2][o][:, cols].bitcast(FP8X4),
                         rhs_scale=slot_scales[e // 2][4 * o : P, cols],
-                        start=(o == 0 and t == 0),
-                        stop=(o == PASSES - 1 and t == PACK - 1),
+                        start=(o == 0 and t == ts[0]),
+                        stop=(o == PASSES - 1 and t == ts[-1]),
                     )
 
         def silu(e):
             for half in range(2):
                 cols = slice(half * HALF, (half + 1) * HALF)
-                nc.scalar.activation(h_bf[e][:, cols, :], banks[(e, half)][:].rearrange("p t n -> p n t"), SILU)
+                if SPLIT2 and e == E - 1 and half == 0:
+                    nc.scalar.activation(h_bf[e][:, cols, :], banks[(e, half)][:].rearrange("p t n -> p n t"), SILU, bias=y_late[:, 0:1])
+                else:
+                    nc.scalar.activation(h_bf[e][:, cols, :], banks[(e, half)][:].rearrange("p t n -> p n t"), SILU)
 
         def second_layer(e, c0, c1):
             nc.vector.quantize_mx(
@@ -191,11 +199,15 @@ def tile_moe_two_mlp_silu_kernel(
 
         def scatter(e, c0, c1, y_ps):
             nc.scalar.copy(y_sb[e][:, c0:c1], y_ps[:])
+            put(e, c0, c1)
+
+        def put(e, c0, c1):
             places = dst_sb[:, (e * C + c0) // 16 : (e * C + c1) // 16]
             nc.vector.tensor_tensor(out_sb[:].indirect(places), y_sb[e][:, c0:c1], gate_sb[:, e * C + c0 : e * C + c1], MULT)
 
         nc.vector.memset(tok_scales[:], 0)
         build_identity()
+        if SPLIT2: nc.vector.memset(y_late, 0.0)
         nc.scalar.activation(warm_out[:], ones[:, 0:16], SILU)
 
         load_words(0)
@@ -217,7 +229,8 @@ def tile_moe_two_mlp_silu_kernel(
         spread_gate()
         gather_scales(0)
         gather_scales(1)
-        cast_w1(nc.scalar.copy, 0, 0, 0, P, 0, PACK)
+        cast_w1(nc.scalar.copy, 0, 0, 0, P - SH00, 0, PACK)
+        if SH00: cast_w1(nc.vector.tensor_copy, 0, 0, P - SH00, P, 0, PACK)
         gather_words(0, 0)
         gather_words(1, 0)
         quantise_w1(0, 0, 0, PACK)
@@ -249,12 +262,21 @@ def tile_moe_two_mlp_silu_kernel(
             quantise_w1(e, 1, 0, 2)
             quantise_w1(e, 1, 2, PACK)
             first_layer(e, 1)
-            scatter(e - 1, 0, C, y_ps)
+            if SPLIT2 and e == E - 1:
+                nc.scalar.copy(y_sb[e - 1][:, 0 : C - 8], y_ps[:, 0 : C - 8])
+                put(e - 1, 0, HALF)
+            else:
+                scatter(e - 1, 0, C, y_ps)
 
         cast_w2(nc.scalar.copy, E - 1)
         quantise_w2(E - 1)
         silu(E - 1)
-        y_halves = [second_layer(E - 1, half * HALF, (half + 1) * HALF) for half in range(2)]
+        if SPLIT2:
+            nc.vector.tensor_copy(y_late[:], y_ps[:, C - 8 : C])
+        y_halves = [second_layer(E - 1, 0, HALF)]
+        if SPLIT2:
+            put(E - 2, HALF, C)
+        y_halves.append(second_layer(E - 1, HALF, C))
         for half in range(2):
             scatter(E - 1, half * HALF, (half + 1) * HALF, y_halves[half])
         nc.sync.dma_start(out=out, in_=out_sb[:])

@@ -33,8 +33,16 @@ VECTOR_SHARE = 56
 LAST_SHARE = 64
 FIRST_PART = 40
 SPLIT2 = 1
-H1ORD = 0
+H1ORD = 1
 SH00 = 0
+WARM1 = 4
+WARM2 = 4
+WARM3 = 0
+SHIFT = 0
+LASTA = 1
+SH30 = 56
+ALT = 0
+SH21 = 56
 
 
 def tile_moe_two_mlp_silu_kernel(
@@ -171,6 +179,20 @@ def tile_moe_two_mlp_silu_kernel(
                         stop=(o == PASSES - 1 and t == ts[-1]),
                     )
 
+        def warm(bank, e, o, count):
+            flat = bank[:].rearrange("p t n -> p (t n)")
+            cols = slice((e % 2) * C, (e % 2 + 1) * C)
+            for i in range(count):
+                nc.tensor.matmul_mx(
+                    out=flat[:, (i % 2) * C : (i % 2 + 1) * C],
+                    lhsT=w1_codes[e][o][:, 3 * P : 4 * P].bitcast(FP8X4),
+                    lhsT_scale=w1_scales[e][o][:, 3 * P : 4 * P],
+                    rhs=slot_words[e // 2][o][:, cols].bitcast(FP8X4),
+                    rhs_scale=slot_scales[e // 2][4 * o : P, cols],
+                    start=True,
+                    stop=True,
+                )
+
         def silu(e):
             for half in range(2):
                 cols = slice(half * HALF, (half + 1) * HALF)
@@ -241,13 +263,26 @@ def tile_moe_two_mlp_silu_kernel(
         first_layer(0, 1)
         gather_words(1, 1)
         for e in range(1, E):
-            scalar_end = P - VECTOR_SHARE
-            cast_w1(nc.scalar.copy, e, 0, 0, UNDER_H // 2, 0, PACK)
-            cast_w1(nc.scalar.copy, e, 0, UNDER_H // 2, UNDER_H, 0, PACK)
-            cast_w1(nc.scalar.copy, e, 0, UNDER_H, scalar_end, 0, 2)
+            scalar_end = P - (VECTOR_SHARE if e < E - 1 else SH30)
+            alt = ALT and e == E - 1
+            if alt:
+                cast_w1(nc.scalar.copy, e, 0, 0, scalar_end, 0, 2)
+                cast_w1(nc.scalar.copy, e, 0, 0, scalar_end - 16, 2, PACK)
+                cast_w1(nc.scalar.copy, e, 0, scalar_end - 16, scalar_end, 2, PACK)
+                cast_w1(nc.vector.tensor_copy, e, 0, scalar_end, P, 0, 2)
+                cast_w1(nc.vector.tensor_copy, e, 0, scalar_end, P - 4, 2, PACK)
+            else:
+                cast_w1(nc.scalar.copy, e, 0, 0, UNDER_H // 2, 0, PACK)
+                cast_w1(nc.scalar.copy, e, 0, UNDER_H // 2, UNDER_H, 0, PACK)
+                cast_w1(nc.scalar.copy, e, 0, UNDER_H, scalar_end, 0, 2)
             silu(e - 1)
-            cast_w1(nc.scalar.copy, e, 0, UNDER_H, scalar_end, 2, PACK)
-            cast_w1(nc.vector.tensor_copy, e, 0, scalar_end, P, 0, PACK)
+            if e == E - 1 and WARM2:
+                warm(banks[(e - 1, 0)], e - 1, 1, WARM2)
+            if alt:
+                cast_w1(nc.scalar.copy, e, 0, P - 4, P, 2, PACK)
+            else:
+                cast_w1(nc.scalar.copy, e, 0, UNDER_H, scalar_end, 2, PACK)
+                cast_w1(nc.vector.tensor_copy, e, 0, scalar_end, P, 0, PACK)
             cast_w2(nc.vector.tensor_copy, e - 1)
             quantise_w2(e - 1)
             quantise_w1(e, 0, 0, 2)
@@ -255,22 +290,42 @@ def tile_moe_two_mlp_silu_kernel(
             quantise_w1(e, 0, 2, PACK)
             first_layer(e, 0)
 
-            scalar_end = P - (VECTOR_SHARE if e < E - 1 else LAST_SHARE)
-            cast_w1(nc.scalar.copy, e, 1, 0, FIRST_PART, 0, PACK)
-            cast_w1(nc.scalar.copy, e, 1, FIRST_PART, scalar_end, 0, PACK)
+            scalar_end = P - (VECTOR_SHARE, SH21, LAST_SHARE)[e - 1]
+            if LASTA and e == E - 1:
+                cast_w1(nc.scalar.copy, e, 1, 0, scalar_end, 0, PACK)
+            else:
+                cast_w1(nc.scalar.copy, e, 1, 0, FIRST_PART, 0, PACK)
+                cast_w1(nc.scalar.copy, e, 1, FIRST_PART, scalar_end, 0, PACK)
             cast_w1(nc.vector.tensor_copy, e, 1, scalar_end, P, 0, PACK)
             quantise_w1(e, 1, 0, 2)
             quantise_w1(e, 1, 2, PACK)
             first_layer(e, 1)
+            if e == E - 2 and WARM1:
+                spare = psum_a.tile([P, PACK, HALF], F32, name="bank")
+                warm(spare, e, 1, WARM1)
             if SPLIT2 and e == E - 1:
+                if SHIFT:
+                    end = LEAD + PACK * H + 8 - C
+                    nc.scalar.copy(stage[E - 1][1][:, end - SHIFT : end], y_prev[:, C - SHIFT : C])
                 nc.scalar.copy(y_sb[e - 1][:, 0 : C - 8], y_ps[:, 0 : C - 8])
-                put(e - 1, 0, HALF)
+                if SHIFT:
+                    c0 = (e - 1) * C - SHIFT
+                    c1 = (e - 1) * C + HALF
+                    nc.vector.tensor_tensor(out_sb[:].indirect(dst_sb[:, c0 // 16 : c1 // 16]), stage[E - 1][1][:, end - SHIFT : end + HALF], gate_sb[:, c0:c1], MULT)
+                else:
+                    put(e - 1, 0, HALF)
+            elif SHIFT and e == E - 2:
+                y_prev = y_ps
+                nc.scalar.copy(y_sb[e - 1][:, SHIFT:C], y_ps[:, 0 : C - SHIFT])
+                nc.vector.tensor_tensor(out_sb[:].indirect(dst_sb[:, (e - 1) * C // 16 : (e * C - SHIFT) // 16]), y_sb[e - 1][:, SHIFT:C], gate_sb[:, (e - 1) * C : e * C - SHIFT], MULT)
             else:
                 scatter(e - 1, 0, C, y_ps)
 
         cast_w2(nc.scalar.copy, E - 1)
         quantise_w2(E - 1)
         silu(E - 1)
+        if WARM3:
+            warm(banks[(E - 1, 0)], E - 1, 1, WARM3)
         if SPLIT2:
             nc.vector.tensor_copy(y_late[:], y_ps[:, C - 8 : C])
         y_halves = [second_layer(E - 1, 0, HALF)]

@@ -35,13 +35,19 @@ FIRST_PART = 40
 SPLIT2 = 1
 H1ORD = 1
 SH00 = 0
-WARM1 = 4
-WARM2 = 4
+WARM1 = 0
+WARM2 = 0
 WARM3 = 0
 SHIFT = 0
 LASTA = 1
 SH30 = 56
 ALT = 0
+WARM0 = 0
+P1A = 0
+P1TAIL = 24
+H1ALL = 0
+SH11 = 56
+QL = 0
 SH21 = 56
 
 
@@ -167,7 +173,7 @@ def tile_moe_two_mlp_silu_kernel(
                 cols = slice((e % 2) * C + half * HALF, (e % 2) * C + (half + 1) * HALF)
                 if o == 0:
                     banks[(e, half)] = psum_a.tile([P, PACK, HALF], F32, name="bank")
-                ts = [2, 3, 0, 1] if (H1ORD and half and o and e == E - 1) else [0, 1, 2, 3]
+                ts = [2, 3, 0, 1] if (H1ORD and half and o and (e == E - 1 or H1ALL)) else [0, 1, 2, 3]
                 for t in ts:
                     nc.tensor.matmul_mx(
                         out=banks[(e, half)][:, t, :],
@@ -276,6 +282,8 @@ def tile_moe_two_mlp_silu_kernel(
                 cast_w1(nc.scalar.copy, e, 0, UNDER_H // 2, UNDER_H, 0, PACK)
                 cast_w1(nc.scalar.copy, e, 0, UNDER_H, scalar_end, 0, 2)
             silu(e - 1)
+            if e == E - 2 and WARM0:
+                warm(banks[(e - 1, 0)], e - 1, 1, WARM0)
             if e == E - 1 and WARM2:
                 warm(banks[(e - 1, 0)], e - 1, 1, WARM2)
             if alt:
@@ -290,15 +298,23 @@ def tile_moe_two_mlp_silu_kernel(
             quantise_w1(e, 0, 2, PACK)
             first_layer(e, 0)
 
-            scalar_end = P - (VECTOR_SHARE, SH21, LAST_SHARE)[e - 1]
+            scalar_end = P - (SH11, SH21, LAST_SHARE)[e - 1]
             if LASTA and e == E - 1:
                 cast_w1(nc.scalar.copy, e, 1, 0, scalar_end, 0, PACK)
+            elif P1A:
+                cast_w1(nc.scalar.copy, e, 1, 0, scalar_end, 0, 2)
+                cast_w1(nc.scalar.copy, e, 1, 0, scalar_end - P1TAIL, 2, PACK)
+                cast_w1(nc.scalar.copy, e, 1, scalar_end - P1TAIL, scalar_end, 2, PACK)
             else:
                 cast_w1(nc.scalar.copy, e, 1, 0, FIRST_PART, 0, PACK)
                 cast_w1(nc.scalar.copy, e, 1, FIRST_PART, scalar_end, 0, PACK)
             cast_w1(nc.vector.tensor_copy, e, 1, scalar_end, P, 0, PACK)
             quantise_w1(e, 1, 0, 2)
-            quantise_w1(e, 1, 2, PACK)
+            if QL and e == E - 1:
+                quantise_w1(e, 1, 2, 3)
+                quantise_w1(e, 1, 3, 4)
+            else:
+                quantise_w1(e, 1, 2, PACK)
             first_layer(e, 1)
             if e == E - 2 and WARM1:
                 spare = psum_a.tile([P, PACK, HALF], F32, name="bank")

@@ -30,25 +30,12 @@ OVERLAP = 16
 UNDER_H = (C + OVERLAP) // PACK
 
 VECTOR_SHARE = 56
-LAST_SHARE = 64
-FIRST_PART = 40
-SPLIT2 = 1
-H1ORD = 1
-SH00 = 0
-WARM1 = 0
-WARM2 = 0
-WARM3 = 0
-SHIFT = 0
-LASTA = 1
-SH30 = 56
-ALT = 0
-WARM0 = 0
-P1A = 0
-P1TAIL = 24
-H1ALL = 0
-SH11 = 56
-QL = 0
 SH21 = 56
+SH30 = 80
+SH31 = 80
+Y_OVERLAP = 4
+FIRST_PART = 40
+LATE = 8
 
 
 def tile_moe_two_mlp_silu_kernel(
@@ -67,7 +54,7 @@ def tile_moe_two_mlp_silu_kernel(
         dst_sb = keep.tile([P, E * LIST_COLS], U16, name="dst_sb")
         tok_scales = sb("tok_scales", [P, T // 4], I32)
         tok_words = [sb("tok_words%d" % o, [P, T], I32) for o in range(PASSES)]
-        stage = [[sb("stage%d_%d" % (e, o), [P, LEAD + PACK * H + 8], F32, "", 256) for o in range(PASSES)] for e in range(E)]
+        stage = [[sb("stage%d_%d" % (e, o), [P, LEAD + PACK * H], F32, "", 256) for o in range(PASSES)] for e in range(E)]
         w1_raw = [[stage[e][o][:, LEAD : LEAD + PACK * H].rearrange("p (j c) -> p j c", j=PACK) for o in range(PASSES)] for e in range(E)]
         w1_bf = [[sb("w1_bf%d_%d" % (e, o), [P, PACK, P, PACK], BF16) for o in range(PASSES)] for e in range(E)]
         w1_codes = [[sb("w1_codes%d_%d" % (e, o), [P, H], U32, "tok_scales" if e + o == 0 else "") for o in range(PASSES)] for e in range(E)]
@@ -90,10 +77,10 @@ def tile_moe_two_mlp_silu_kernel(
         h_bf.append(sb("h_bf", [P, C, PACK], BF16))
         h_codes = [sb("h_codes%d" % e, [P, C], U32) for e in range(E)]
         h_scales = [sb("h_scales%d" % e, [P, C], U8) for e in range(E)]
-        y_sb = [stage[e + 1][1][:, OVERLAP : OVERLAP + C] for e in range(E - 2)]
-        y_sb.append(stage[E - 1][1][:, LEAD + PACK * H + 8 - C : LEAD + PACK * H + 8])
+        y_sb = [stage[1][1][:, OVERLAP : OVERLAP + C]]
+        y_sb.extend(stage[e + 1][1][:, Y_OVERLAP : Y_OVERLAP + C] for e in range(1, E - 1))
         y_sb.append(sb("y_sb", [P, C], F32))
-        y_late = stage[E - 1][1][:, LEAD + PACK * H : LEAD + PACK * H + 8]
+        y_late = y_sb[1][:, 0:LATE]
         out_sb = sb("out_sb", [P, T], F32)
         warm_out = sb("warm_out", [P, 16], F32)
 
@@ -173,7 +160,7 @@ def tile_moe_two_mlp_silu_kernel(
                 cols = slice((e % 2) * C + half * HALF, (e % 2) * C + (half + 1) * HALF)
                 if o == 0:
                     banks[(e, half)] = psum_a.tile([P, PACK, HALF], F32, name="bank")
-                ts = [2, 3, 0, 1] if (H1ORD and half and o and (e == E - 1 or H1ALL)) else [0, 1, 2, 3]
+                ts = [2, 3, 0, 1] if half and o and e == E - 1 else [0, 1, 2, 3]
                 for t in ts:
                     nc.tensor.matmul_mx(
                         out=banks[(e, half)][:, t, :],
@@ -185,24 +172,10 @@ def tile_moe_two_mlp_silu_kernel(
                         stop=(o == PASSES - 1 and t == ts[-1]),
                     )
 
-        def warm(bank, e, o, count):
-            flat = bank[:].rearrange("p t n -> p (t n)")
-            cols = slice((e % 2) * C, (e % 2 + 1) * C)
-            for i in range(count):
-                nc.tensor.matmul_mx(
-                    out=flat[:, (i % 2) * C : (i % 2 + 1) * C],
-                    lhsT=w1_codes[e][o][:, 3 * P : 4 * P].bitcast(FP8X4),
-                    lhsT_scale=w1_scales[e][o][:, 3 * P : 4 * P],
-                    rhs=slot_words[e // 2][o][:, cols].bitcast(FP8X4),
-                    rhs_scale=slot_scales[e // 2][4 * o : P, cols],
-                    start=True,
-                    stop=True,
-                )
-
         def silu(e):
             for half in range(2):
                 cols = slice(half * HALF, (half + 1) * HALF)
-                if SPLIT2 and e == E - 1 and half == 0:
+                if e == E - 1 and half == 0:
                     nc.scalar.activation(h_bf[e][:, cols, :], banks[(e, half)][:].rearrange("p t n -> p n t"), SILU, bias=y_late[:, 0:1])
                 else:
                     nc.scalar.activation(h_bf[e][:, cols, :], banks[(e, half)][:].rearrange("p t n -> p n t"), SILU)
@@ -235,7 +208,7 @@ def tile_moe_two_mlp_silu_kernel(
 
         nc.vector.memset(tok_scales[:], 0)
         build_identity()
-        if SPLIT2: nc.vector.memset(y_late, 0.0)
+        nc.vector.memset(y_late, 0.0)
         nc.scalar.activation(warm_out[:], ones[:, 0:16], SILU)
 
         load_words(0)
@@ -257,8 +230,7 @@ def tile_moe_two_mlp_silu_kernel(
         spread_gate()
         gather_scales(0)
         gather_scales(1)
-        cast_w1(nc.scalar.copy, 0, 0, 0, P - SH00, 0, PACK)
-        if SH00: cast_w1(nc.vector.tensor_copy, 0, 0, P - SH00, P, 0, PACK)
+        cast_w1(nc.scalar.copy, 0, 0, 0, P, 0, PACK)
         gather_words(0, 0)
         gather_words(1, 0)
         quantise_w1(0, 0, 0, PACK)
@@ -268,29 +240,14 @@ def tile_moe_two_mlp_silu_kernel(
         quantise_w1(0, 1, 0, PACK)
         first_layer(0, 1)
         gather_words(1, 1)
-        for e in range(1, E):
-            scalar_end = P - (VECTOR_SHARE if e < E - 1 else SH30)
-            alt = ALT and e == E - 1
-            if alt:
-                cast_w1(nc.scalar.copy, e, 0, 0, scalar_end, 0, 2)
-                cast_w1(nc.scalar.copy, e, 0, 0, scalar_end - 16, 2, PACK)
-                cast_w1(nc.scalar.copy, e, 0, scalar_end - 16, scalar_end, 2, PACK)
-                cast_w1(nc.vector.tensor_copy, e, 0, scalar_end, P, 0, 2)
-                cast_w1(nc.vector.tensor_copy, e, 0, scalar_end, P - 4, 2, PACK)
-            else:
-                cast_w1(nc.scalar.copy, e, 0, 0, UNDER_H // 2, 0, PACK)
-                cast_w1(nc.scalar.copy, e, 0, UNDER_H // 2, UNDER_H, 0, PACK)
-                cast_w1(nc.scalar.copy, e, 0, UNDER_H, scalar_end, 0, 2)
+        for e in range(1, E - 1):
+            scalar_end = P - VECTOR_SHARE
+            cast_w1(nc.scalar.copy, e, 0, 0, UNDER_H // 2, 0, PACK)
+            cast_w1(nc.scalar.copy, e, 0, UNDER_H // 2, UNDER_H, 0, PACK)
+            cast_w1(nc.scalar.copy, e, 0, UNDER_H, scalar_end, 0, 2)
             silu(e - 1)
-            if e == E - 2 and WARM0:
-                warm(banks[(e - 1, 0)], e - 1, 1, WARM0)
-            if e == E - 1 and WARM2:
-                warm(banks[(e - 1, 0)], e - 1, 1, WARM2)
-            if alt:
-                cast_w1(nc.scalar.copy, e, 0, P - 4, P, 2, PACK)
-            else:
-                cast_w1(nc.scalar.copy, e, 0, UNDER_H, scalar_end, 2, PACK)
-                cast_w1(nc.vector.tensor_copy, e, 0, scalar_end, P, 0, PACK)
+            cast_w1(nc.scalar.copy, e, 0, UNDER_H, scalar_end, 2, PACK)
+            cast_w1(nc.vector.tensor_copy, e, 0, scalar_end, P, 0, PACK)
             cast_w2(nc.vector.tensor_copy, e - 1)
             quantise_w2(e - 1)
             quantise_w1(e, 0, 0, 2)
@@ -298,55 +255,45 @@ def tile_moe_two_mlp_silu_kernel(
             quantise_w1(e, 0, 2, PACK)
             first_layer(e, 0)
 
-            scalar_end = P - (SH11, SH21, LAST_SHARE)[e - 1]
-            if LASTA and e == E - 1:
-                cast_w1(nc.scalar.copy, e, 1, 0, scalar_end, 0, PACK)
-            elif P1A:
-                cast_w1(nc.scalar.copy, e, 1, 0, scalar_end, 0, 2)
-                cast_w1(nc.scalar.copy, e, 1, 0, scalar_end - P1TAIL, 2, PACK)
-                cast_w1(nc.scalar.copy, e, 1, scalar_end - P1TAIL, scalar_end, 2, PACK)
-            else:
+            if e == 1:
                 cast_w1(nc.scalar.copy, e, 1, 0, FIRST_PART, 0, PACK)
                 cast_w1(nc.scalar.copy, e, 1, FIRST_PART, scalar_end, 0, PACK)
+            else:
+                scalar_end = P - SH21
+                cast_w1(nc.scalar.copy, e, 1, 0, scalar_end, 0, PACK)
             cast_w1(nc.vector.tensor_copy, e, 1, scalar_end, P, 0, PACK)
             quantise_w1(e, 1, 0, 2)
-            if QL and e == E - 1:
-                quantise_w1(e, 1, 2, 3)
-                quantise_w1(e, 1, 3, 4)
-            else:
-                quantise_w1(e, 1, 2, PACK)
+            quantise_w1(e, 1, 2, PACK)
             first_layer(e, 1)
-            if e == E - 2 and WARM1:
-                spare = psum_a.tile([P, PACK, HALF], F32, name="bank")
-                warm(spare, e, 1, WARM1)
-            if SPLIT2 and e == E - 1:
-                if SHIFT:
-                    end = LEAD + PACK * H + 8 - C
-                    nc.scalar.copy(stage[E - 1][1][:, end - SHIFT : end], y_prev[:, C - SHIFT : C])
-                nc.scalar.copy(y_sb[e - 1][:, 0 : C - 8], y_ps[:, 0 : C - 8])
-                if SHIFT:
-                    c0 = (e - 1) * C - SHIFT
-                    c1 = (e - 1) * C + HALF
-                    nc.vector.tensor_tensor(out_sb[:].indirect(dst_sb[:, c0 // 16 : c1 // 16]), stage[E - 1][1][:, end - SHIFT : end + HALF], gate_sb[:, c0:c1], MULT)
-                else:
-                    put(e - 1, 0, HALF)
-            elif SHIFT and e == E - 2:
-                y_prev = y_ps
-                nc.scalar.copy(y_sb[e - 1][:, SHIFT:C], y_ps[:, 0 : C - SHIFT])
-                nc.vector.tensor_tensor(out_sb[:].indirect(dst_sb[:, (e - 1) * C // 16 : (e * C - SHIFT) // 16]), y_sb[e - 1][:, SHIFT:C], gate_sb[:, (e - 1) * C : e * C - SHIFT], MULT)
+            if e == 1:
+                scatter(0, 0, C, y_ps)
             else:
-                scatter(e - 1, 0, C, y_ps)
+                nc.scalar.copy(y_sb[1][:, LATE:C], y_ps[:, LATE:C])
+                put(1, HALF, C)
+        y_held = y_ps
+
+        cast_w1(nc.scalar.copy, 3, 0, 0, P - SH30, 0, PACK)
+        cast_w1(nc.vector.tensor_copy, 3, 0, P - SH30, P, 0, PACK)
+        silu(2)
+        cast_w2(nc.vector.tensor_copy, 2)
+        quantise_w1(3, 0, 0, 2)
+        quantise_w2(2)
+        quantise_w1(3, 0, 2, PACK)
+        first_layer(3, 0)
+        y_ps = second_layer(2, 0, C)
+        cast_w1(nc.scalar.copy, 3, 1, 0, P - SH31, 0, PACK)
+        cast_w1(nc.vector.tensor_copy, 3, 1, P - SH31, P, 0, PACK)
+        quantise_w1(3, 1, 0, 2)
+        quantise_w1(3, 1, 2, PACK)
+        first_layer(3, 1)
+        scatter(2, 0, C, y_ps)
 
         cast_w2(nc.scalar.copy, E - 1)
         quantise_w2(E - 1)
         silu(E - 1)
-        if WARM3:
-            warm(banks[(E - 1, 0)], E - 1, 1, WARM3)
-        if SPLIT2:
-            nc.vector.tensor_copy(y_late[:], y_ps[:, C - 8 : C])
+        nc.vector.tensor_copy(y_late, y_held[:, 0:LATE])
         y_halves = [second_layer(E - 1, 0, HALF)]
-        if SPLIT2:
-            put(E - 2, HALF, C)
+        put(1, 0, HALF)
         y_halves.append(second_layer(E - 1, HALF, C))
         for half in range(2):
             scatter(E - 1, half * HALF, (half + 1) * HALF, y_halves[half])

@@ -31,8 +31,8 @@ UNDER_H = (C + OVERLAP) // PACK
 
 VECTOR_SHARE = 56
 SH21 = 56
-SH30 = 80
-SH31 = 80
+SH30 = 68
+SH31 = 84
 Y_OVERLAP = 4
 FIRST_PART = 40
 LATE = 8
@@ -129,8 +129,8 @@ def tile_moe_two_mlp_silu_kernel(
         def cast_w1(copy, e, o, m0, m1, t0, t1):
             for a in range(t0 // 2, t1 // 2):
                 copy(
-                    w1_bf[e][o][:, 2 * a : 2 * a + 2, m0:m1, :].rearrange("p b (g u) j -> p g j u b", u=2),
-                    w1_raw[e][o][:, :, PACK * m0 : PACK * m1].rearrange("p j (g a u b) -> p a g j u b", a=2, u=2, b=2)[:, a],
+                    w1_bf[e][o][:, 2 * a : 2 * a + 2, m0:m1, :].rearrange("p b (g u) j -> p g j b u", u=2),
+                    w1_raw[e][o][:, :, PACK * m0 : PACK * m1].rearrange("p j (g a u b) -> p a g j b u", a=2, u=2, b=2)[:, a],
                 )
 
         def quantise_w1(e, o, t0, t1):
@@ -160,7 +160,7 @@ def tile_moe_two_mlp_silu_kernel(
                 cols = slice((e % 2) * C + half * HALF, (e % 2) * C + (half + 1) * HALF)
                 if o == 0:
                     banks[(e, half)] = psum_a.tile([P, PACK, HALF], F32, name="bank")
-                ts = [2, 3, 0, 1] if half and o and e == E - 1 else [0, 1, 2, 3]
+                ts = [3, 2, 0, 1] if half and o and e == E - 1 else [0, 1, 2, 3]
                 for t in ts:
                     nc.tensor.matmul_mx(
                         out=banks[(e, half)][:, t, :],
@@ -284,7 +284,8 @@ def tile_moe_two_mlp_silu_kernel(
         cast_w1(nc.scalar.copy, 3, 1, 0, P - SH31, 0, PACK)
         cast_w1(nc.vector.tensor_copy, 3, 1, P - SH31, P, 0, PACK)
         quantise_w1(3, 1, 0, 2)
-        quantise_w1(3, 1, 2, PACK)
+        quantise_w1(3, 1, 2, 3)
+        quantise_w1(3, 1, 3, PACK)
         first_layer(3, 1)
         scatter(2, 0, C, y_ps)
 

@@ -47,7 +47,7 @@ def tile_moe_two_mlp_silu_kernel(
         psum_a = ctx.enter_context(tc.psum_pool(name="psum_a", bufs=6))
         psum_y = ctx.enter_context(tc.psum_pool(name="psum_y", bufs=2))
 
-        def sb(name, shape, dtype, tag="", align=64):
+        def sb(name, shape, dtype, tag="", align=256):
             return keep.tile(shape, dtype, name=name, tag=tag or name, align_bytes=align)
 
         offs_sb = keep.tile([P, E * LIST_COLS], U16, name="offs_sb")

@@ -16,6 +16,7 @@ SILU = mybir.ActivationFunctionType.Silu
 MULT = mybir.AluOpType.mult
 ADD = mybir.AluOpType.add
 EQUAL = mybir.AluOpType.is_equal
+COPY = mybir.ActivationFunctionType.Copy
 
 P = 128
 PACK = 4
@@ -31,11 +32,9 @@ UNDER_H = (C + OVERLAP) // PACK
 
 VECTOR_SHARE = 56
 SH21 = 56
-SH30 = 68
 SH31 = 84
 Y_OVERLAP = 4
 FIRST_PART = 40
-LATE = 8
 
 
 def tile_moe_two_mlp_silu_kernel(
@@ -56,7 +55,8 @@ def tile_moe_two_mlp_silu_kernel(
         tok_words = [sb("tok_words%d" % o, [P, T], I32) for o in range(PASSES)]
         stage = [[sb("stage%d_%d" % (e, o), [P, LEAD + PACK * H], F32, "", 256) for o in range(PASSES)] for e in range(E)]
         w1_raw = [[stage[e][o][:, LEAD : LEAD + PACK * H].rearrange("p (j c) -> p j c", j=PACK) for o in range(PASSES)] for e in range(E)]
-        w1_bf = [[sb("w1_bf%d_%d" % (e, o), [P, PACK, P, PACK], BF16) for o in range(PASSES)] for e in range(E)]
+        w1_bf = [[sb("w1_bf%d_%d" % (e, o), [P, PACK, P, PACK], BF16) if (e, o) != (E - 1, 0) else None for o in range(PASSES)] for e in range(E)]
+        pair_bf = [sb("pair_bf%d" % a, [P, 2, P, PACK], BF16) for a in range(2)]
         w1_codes = [[sb("w1_codes%d_%d" % (e, o), [P, H], U32, "tok_scales" if e + o == 0 else "") for o in range(PASSES)] for e in range(E)]
         w1_scales = [[sb("w1_scales%d_%d" % (e, o), [P, H], U8) for o in range(PASSES)] for e in range(E)]
         w2_raw = [sb("w2_raw%d" % e, [P, PACK, N], F32) for e in range(E)]
@@ -73,14 +73,14 @@ def tile_moe_two_mlp_silu_kernel(
             [sb("slot_words%d_%d" % (g, o), [P, 2 * C], U32, "w1_bf0_1" if g and o else "") for o in range(PASSES)] for g in range(E // 2)
         ]
         slot_scales = [sb("slot_scales%d" % g, [P, 2 * C], U8) for g in range(E // 2)]
-        h_bf = [stage[e + 1][0][:, OVERLAP : OVERLAP + 2 * C].bitcast(BF16).rearrange("p (n t) -> p n t", t=PACK) for e in range(E - 1)]
-        h_bf.append(sb("h_bf", [P, C, PACK], BF16))
-        h_codes = [sb("h_codes%d" % e, [P, C], U32) for e in range(E)]
+        h_bf = [stage[e + 1][0][:, OVERLAP : OVERLAP + 2 * C].bitcast(BF16).rearrange("p (n t) -> p n t", t=PACK) for e in range(E - 2)]
+        h_bf.extend(sb("h_bf%d" % e, [P, C, PACK], BF16) for e in range(E - 2, E))
+        h_codes = [sb("h_codes%d" % e, [P, C], U32, "pair_bf1" if e == 2 else "") for e in range(E)]
         h_scales = [sb("h_scales%d" % e, [P, C], U8) for e in range(E)]
         y_sb = [stage[1][1][:, OVERLAP : OVERLAP + C]]
         y_sb.extend(stage[e + 1][1][:, Y_OVERLAP : Y_OVERLAP + C] for e in range(1, E - 1))
         y_sb.append(sb("y_sb", [P, C], F32))
-        y_late = y_sb[1][:, 0:LATE]
+        y_gated = stage[E - 1][0][:, LEAD : LEAD + HALF]
         out_sb = sb("out_sb", [P, T], F32)
         warm_out = sb("warm_out", [P, 16], F32)
 
@@ -133,6 +133,19 @@ def tile_moe_two_mlp_silu_kernel(
                     w1_raw[e][o][:, :, PACK * m0 : PACK * m1].rearrange("p j (g a u b) -> p a g j b u", a=2, u=2, b=2)[:, a],
                 )
 
+        def cast_pair(copy, a, m0, m1):
+            copy(
+                pair_bf[a][:, :, m0:m1, :].rearrange("p b (g u) j -> p g j b u", u=2),
+                w1_raw[E - 1][0][:, :, PACK * m0 : PACK * m1].rearrange("p j (g a u b) -> p a g j b u", a=2, u=2, b=2)[:, a],
+            )
+
+        def quantise_pair(a):
+            nc.vector.quantize_mx(
+                out=w1_codes[E - 1][0][:, 2 * a * P : 2 * (a + 1) * P].bitcast(FP8X4),
+                scales=w1_scales[E - 1][0][:, 2 * a * P : 2 * (a + 1) * P],
+                in_=pair_bf[a][:].rearrange("p t m j -> p (t m j)"),
+            )
+
         def quantise_w1(e, o, t0, t1):
             nc.vector.quantize_mx(
                 out=w1_codes[e][o][:, t0 * P : t1 * P].bitcast(FP8X4),
@@ -160,7 +173,9 @@ def tile_moe_two_mlp_silu_kernel(
                 cols = slice((e % 2) * C + half * HALF, (e % 2) * C + (half + 1) * HALF)
                 if o == 0:
                     banks[(e, half)] = psum_a.tile([P, PACK, HALF], F32, name="bank")
-                ts = [3, 2, 0, 1] if half and o and e == E - 1 else [0, 1, 2, 3]
+                ts = [0, 1, 2, 3]
+                if e == E - 1:
+                    ts = [2, 3, 0, 1] if o == 0 else [3, 2, 0, 1] if half else ts
                 for t in ts:
                     nc.tensor.matmul_mx(
                         out=banks[(e, half)][:, t, :],
@@ -175,10 +190,7 @@ def tile_moe_two_mlp_silu_kernel(
         def silu(e):
             for half in range(2):
                 cols = slice(half * HALF, (half + 1) * HALF)
-                if e == E - 1 and half == 0:
-                    nc.scalar.activation(h_bf[e][:, cols, :], banks[(e, half)][:].rearrange("p t n -> p n t"), SILU, bias=y_late[:, 0:1])
-                else:
-                    nc.scalar.activation(h_bf[e][:, cols, :], banks[(e, half)][:].rearrange("p t n -> p n t"), SILU)
+                nc.scalar.activation(h_bf[e][:, cols, :], banks[(e, half)][:].rearrange("p t n -> p n t"), SILU)
 
         def second_layer(e, c0, c1):
             nc.vector.quantize_mx(
@@ -208,7 +220,6 @@ def tile_moe_two_mlp_silu_kernel(
 
         nc.vector.memset(tok_scales[:], 0)
         build_identity()
-        nc.vector.memset(y_late, 0.0)
         nc.scalar.activation(warm_out[:], ones[:, 0:16], SILU)
 
         load_words(0)
@@ -220,8 +231,11 @@ def tile_moe_two_mlp_silu_kernel(
         load_w1(0, 1)
         load_words(1)
         for e in range(1, E):
+            if e == E - 1:
+                load_w2(e - 1)
             load_w1(e, 0)
-            load_w2(e - 1)
+            if e < E - 1:
+                load_w2(e - 1)
             if e == 1:
                 nc.sync.dma_start(dst_sb[:], dst)
             load_w1(e, 1)
@@ -268,19 +282,21 @@ def tile_moe_two_mlp_silu_kernel(
             if e == 1:
                 scatter(0, 0, C, y_ps)
             else:
-                nc.scalar.copy(y_sb[1][:, LATE:C], y_ps[:, LATE:C])
+                nc.scalar.copy(y_sb[1][:, HALF:C], y_ps[:, HALF:C])
                 put(1, HALF, C)
         y_held = y_ps
 
-        cast_w1(nc.scalar.copy, 3, 0, 0, P - SH30, 0, PACK)
-        cast_w1(nc.vector.tensor_copy, 3, 0, P - SH30, P, 0, PACK)
-        silu(2)
-        cast_w2(nc.vector.tensor_copy, 2)
-        quantise_w1(3, 0, 0, 2)
+        cast_w2(nc.scalar.copy, 2)
         quantise_w2(2)
-        quantise_w1(3, 0, 2, PACK)
-        first_layer(3, 0)
+        silu(2)
+        cast_pair(nc.vector.tensor_copy, 1, 0, P)
+        cast_pair(nc.vector.tensor_copy, 0, 0, P)
+        nc.vector.tensor_tensor(y_gated, y_held[:, 0:HALF], gate_sb[:, C : C + HALF], MULT)
+        nc.scalar.activation(out_sb[:].indirect(dst_sb[:, C // 16 : (C + HALF) // 16]), y_gated, COPY)
+        quantise_pair(1)
+        quantise_pair(0)
         y_ps = second_layer(2, 0, C)
+        first_layer(3, 0)
         cast_w1(nc.scalar.copy, 3, 1, 0, P - SH31, 0, PACK)
         cast_w1(nc.vector.tensor_copy, 3, 1, P - SH31, P, 0, PACK)
         quantise_w1(3, 1, 0, 2)
@@ -292,10 +308,7 @@ def tile_moe_two_mlp_silu_kernel(
         cast_w2(nc.scalar.copy, E - 1)
         quantise_w2(E - 1)
         silu(E - 1)
-        nc.vector.tensor_copy(y_late, y_held[:, 0:LATE])
-        y_halves = [second_layer(E - 1, 0, HALF)]
-        put(1, 0, HALF)
-        y_halves.append(second_layer(E - 1, HALF, C))
+        y_halves = [second_layer(E - 1, half * HALF, (half + 1) * HALF) for half in range(2)]
         for half in range(2):
             scatter(E - 1, half * HALF, (half + 1) * HALF, y_halves[half])
         nc.sync.dma_start(out=out, in_=out_sb[:])

@@ -31,8 +31,8 @@ OVERLAP = 16
 UNDER_H = (C + OVERLAP) // PACK
 
 VECTOR_SHARE = 56
-SH21 = 56
-SH31 = 84
+SH21 = 72
+SH31 = 80
 Y_OVERLAP = 4
 FIRST_PART = 40
 
@@ -80,7 +80,7 @@ def tile_moe_two_mlp_silu_kernel(
         y_sb = [stage[1][1][:, OVERLAP : OVERLAP + C]]
         y_sb.extend(stage[e + 1][1][:, Y_OVERLAP : Y_OVERLAP + C] for e in range(1, E - 1))
         y_sb.append(sb("y_sb", [P, C], F32))
-        y_gated = stage[E - 1][0][:, LEAD : LEAD + HALF]
+        y_gated = w2_raw[2][:, 0, :]
         out_sb = sb("out_sb", [P, T], F32)
         warm_out = sb("warm_out", [P, 16], F32)
 
@@ -288,11 +288,11 @@ def tile_moe_two_mlp_silu_kernel(
 
         cast_w2(nc.scalar.copy, 2)
         quantise_w2(2)
+        nc.vector.tensor_tensor(y_gated, y_held[:, 0:HALF], gate_sb[:, C : C + HALF], MULT)
         silu(2)
+        nc.scalar.activation(out_sb[:].indirect(dst_sb[:, C // 16 : (C + HALF) // 16]), y_gated, COPY)
         cast_pair(nc.vector.tensor_copy, 1, 0, P)
         cast_pair(nc.vector.tensor_copy, 0, 0, P)
-        nc.vector.tensor_tensor(y_gated, y_held[:, 0:HALF], gate_sb[:, C : C + HALF], MULT)
-        nc.scalar.activation(out_sb[:].indirect(dst_sb[:, C // 16 : (C + HALF) // 16]), y_gated, COPY)
         quantise_pair(1)
         quantise_pair(0)
         y_ps = second_layer(2, 0, C)

from contextlib import ExitStack

import concourse.mybir as mybir

K, T, E, C, H, N = 1024, 1024, 4, 256, 512, 128
FLOPS = 2 * E * C * (K * H + H * N)

F32 = mybir.dt.float32
BF16 = mybir.dt.bfloat16
I32 = mybir.dt.int32
U32 = mybir.dt.uint32
U16 = mybir.dt.uint16
U8 = mybir.dt.uint8
FP8X4 = mybir.dt.float8_e4m3fn_x4
SILU = mybir.ActivationFunctionType.Silu
MULT = mybir.AluOpType.mult
ADD = mybir.AluOpType.add
EQUAL = mybir.AluOpType.is_equal
COPY = mybir.ActivationFunctionType.Copy

P = 128
PACK = 4
K_PASS = P * PACK
PASSES = K // K_PASS
HALF = C // 2
LIST_COLS = C // 16
QUADRANT = 32

LEAD = C
OVERLAP = 16
UNDER_H = (C + OVERLAP) // PACK

VECTOR_SHARE = 56
SH21 = 72
SH31 = 80
Y_OVERLAP = 4
FIRST_PART = 40


def tile_moe_two_mlp_silu_kernel(
    tc, x_words, x_scales, w1, w2, gate, offs, dst, out
):
    nc = tc.nc
    with ExitStack() as ctx:
        keep = ctx.enter_context(tc.tile_pool(name="keep", bufs=1))
        psum_a = ctx.enter_context(tc.psum_pool(name="psum_a", bufs=6))
        psum_y = ctx.enter_context(tc.psum_pool(name="psum_y", bufs=2))

        def sb(name, shape, dtype, tag="", align=256):
            return keep.tile(shape, dtype, name=name, tag=tag or name, align_bytes=align)

        offs_sb = keep.tile([P, E * LIST_COLS], U16, name="offs_sb")
        dst_sb = keep.tile([P, E * LIST_COLS], U16, name="dst_sb")
        tok_scales = sb("tok_scales", [P, T // 4], I32)
        tok_words = [sb("tok_words%d" % o, [P, T], I32) for o in range(PASSES)]
        stage = [[sb("stage%d_%d" % (e, o), [P, LEAD + PACK * H], F32, "", 256) for o in range(PASSES)] for e in range(E)]
        w1_raw = [[stage[e][o][:, LEAD : LEAD + PACK * H].rearrange("p (j c) -> p j c", j=PACK) for o in range(PASSES)] for e in range(E)]
        w1_bf = [[sb("w1_bf%d_%d" % (e, o), [P, PACK, P, PACK], BF16) if (e, o) != (E - 1, 0) else None for o in range(PASSES)] for e in range(E)]
        pair_bf = [sb("pair_bf%d" % a, [P, 2, P, PACK], BF16) for a in range(2)]
        w1_codes = [[sb("w1_codes%d_%d" % (e, o), [P, H], U32, "tok_scales" if e + o == 0 else "") for o in range(PASSES)] for e in range(E)]
        w1_scales = [[sb("w1_scales%d_%d" % (e, o), [P, H], U8) for o in range(PASSES)] for e in range(E)]
        w2_raw = [sb("w2_raw%d" % e, [P, PACK, N], F32) for e in range(E)]
        w2_bf = [sb("w2_bf%d" % e, [P, N, PACK], BF16) for e in range(E)]
        w2_codes = [sb("w2_codes%d" % e, [P, N], U32) for e in range(E)]
        w2_scales = [sb("w2_scales%d" % e, [P, N], U8) for e in range(E)]
        gate_col = sb("gate_col", [P, T // P], F32)
        gate_sb = sb("gate_sb", [P, T], F32)
        identity = sb("identity", [P, P], F32)
        ones = sb("ones", [P, QUADRANT], F32)
        column = sb("column", [P, QUADRANT], F32)
        row = sb("row", [P, QUADRANT], F32)
        slot_words = [
            [sb("slot_words%d_%d" % (g, o), [P, 2 * C], U32, "w1_bf0_1" if g and o else "") for o in range(PASSES)] for g in range(E // 2)
        ]
        slot_scales = [sb("slot_scales%d" % g, [P, 2 * C], U8) for g in range(E // 2)]
        h_bf = [stage[e + 1][0][:, OVERLAP : OVERLAP + 2 * C].bitcast(BF16).rearrange("p (n t) -> p n t", t=PACK) for e in range(E - 2)]
        h_bf.extend(sb("h_bf%d" % e, [P, C, PACK], BF16) for e in range(E - 2, E))
        h_codes = [sb("h_codes%d" % e, [P, C], U32, "pair_bf1" if e == 2 else "") for e in range(E)]
        h_scales = [sb("h_scales%d" % e, [P, C], U8) for e in range(E)]
        y_sb = [stage[1][1][:, OVERLAP : OVERLAP + C]]
        y_sb.extend(stage[e + 1][1][:, Y_OVERLAP : Y_OVERLAP + C] for e in range(1, E - 1))
        y_sb.append(sb("y_sb", [P, C], F32))
        y_gated = w2_raw[2][:, 0, :]
        out_sb = sb("out_sb", [P, T], F32)
        warm_out = sb("warm_out", [P, 16], F32)

        def load_w1(e, o):
            rows = w1[e, o * K_PASS : (o + 1) * K_PASS, :].rearrange("(p j) c -> p j c", j=PACK)
            nc.sync.dma_start(out=w1_raw[e][o], in_=rows)

        def load_words(o):
            nc.sync.dma_start(out=tok_words[o][:], in_=x_words[o].rearrange("p t r -> p (t r)").bitcast(I32))

        def load_w2(e):
            rows = w2[e].rearrange("(g a u b) n -> a g u (b n)", a=2, u=2, b=2)
            for a in range(2):
                nc.sync.dma_start(out=w2_raw[e][:, 2 * a : 2 * a + 2, :].rearrange("p b n -> p (b n)"), in_=rows[a])

        def load_scales(o):
            for r in range(4):
                nc.sync.dma_start(out=tok_scales[4 * o + r : P : QUADRANT, :], in_=x_scales[o, r:16:4, :].bitcast(I32))

        def build_identity():
            nc.vector.memset(ones[:], 1.0)
            nc.vector.memset(identity[:], 0.0)
            nc.vector.tensor_tensor_scan(column[:], ones[:], ones[:], 0.0, MULT, ADD)
            nc.vector.transpose(row[:], column[:])
            for p0 in range(0, P, QUADRANT):
                part = slice(p0, p0 + QUADRANT)
                nc.vector.tensor_tensor(identity[part, part], row[part, :], column[part, :], EQUAL)

        def spread_gate():
            by_column = gate_sb[:].rearrange("p (s c) -> p s c", s=P)
            for c0 in range(0, T // P, PACK):
                spread = psum_y.tile([P, PACK, P], F32, name="y_ps")
                for c in range(PACK):
                    nc.tensor.transpose(spread[:, c, :], gate_col[:, c0 + c : c0 + c + 1].to_broadcast([P, P]), identity[:])
                nc.scalar.copy(by_column[:, :, c0 : c0 + PACK], spread[:].rearrange("p c s -> p s c"))

        def pair_list(g):
            return offs_sb[:, 2 * g * LIST_COLS : 2 * (g + 1) * LIST_COLS]

        def gather_scales(g):
            nc.vector.tensor_copy(slot_scales[g][:], tok_scales[:].bitcast(U8).indirect(pair_list(g)))

        def gather_words(g, o):
            nc.vector.tensor_copy(slot_words[g][o][:], tok_words[o][:].bitcast(U32).indirect(pair_list(g)))

        def cast_w1(copy, e, o, m0, m1, t0, t1):
            for a in range(t0 // 2, t1 // 2):
                copy(
                    w1_bf[e][o][:, 2 * a : 2 * a + 2, m0:m1, :].rearrange("p b (g u) j -> p g j b u", u=2),
                    w1_raw[e][o][:, :, PACK * m0 : PACK * m1].rearrange("p j (g a u b) -> p a g j b u", a=2, u=2, b=2)[:, a],
                )

        def cast_pair(copy, a, m0, m1):
            copy(
                pair_bf[a][:, :, m0:m1, :].rearrange("p b (g u) j -> p g j b u", u=2),
                w1_raw[E - 1][0][:, :, PACK * m0 : PACK * m1].rearrange("p j (g a u b) -> p a g j b u", a=2, u=2, b=2)[:, a],
            )

        def quantise_pair(a):
            nc.vector.quantize_mx(
                out=w1_codes[E - 1][0][:, 2 * a * P : 2 * (a + 1) * P].bitcast(FP8X4),
                scales=w1_scales[E - 1][0][:, 2 * a * P : 2 * (a + 1) * P],
                in_=pair_bf[a][:].rearrange("p t m j -> p (t m j)"),
            )

        def quantise_w1(e, o, t0, t1):
            nc.vector.quantize_mx(
                out=w1_codes[e][o][:, t0 * P : t1 * P].bitcast(FP8X4),
                scales=w1_scales[e][o][:, t0 * P : t1 * P],
                in_=w1_bf[e][o][:, t0:t1, :, :].rearrange("p t m j -> p (t m j)"),
            )

        def cast_w2(copy, e):
            copy(
                w2_bf[e][:].rearrange("p (c i) j -> p c j i", i=4),
                w2_raw[e][:].rearrange("p j (c i) -> p c j i", i=4),
            )

        def quantise_w2(e):
            nc.vector.quantize_mx(
                out=w2_codes[e][:].bitcast(FP8X4),
                scales=w2_scales[e][:],
                in_=w2_bf[e][:].rearrange("p n j -> p (n j)"),
            )

        banks = {}

        def first_layer(e, o):
            for half in range(2):
                cols = slice((e % 2) * C + half * HALF, (e % 2) * C + (half + 1) * HALF)
                if o == 0:
                    banks[(e, half)] = psum_a.tile([P, PACK, HALF], F32, name="bank")
                ts = [0, 1, 2, 3]
                if e == E - 1:
                    ts = [2, 3, 0, 1] if o == 0 else [3, 2, 0, 1] if half else ts
                for t in ts:
                    nc.tensor.matmul_mx(
                        out=banks[(e, half)][:, t, :],
                        lhsT=w1_codes[e][o][:, t * P : (t + 1) * P].bitcast(FP8X4),
                        lhsT_scale=w1_scales[e][o][:, t * P : (t + 1) * P],
                        rhs=slot_words[e // 2][o][:, cols].bitcast(FP8X4),
                        rhs_scale=slot_scales[e // 2][4 * o : P, cols],
                        start=(o == 0 and t == ts[0]),
                        stop=(o == PASSES - 1 and t == ts[-1]),
                    )

        def silu(e):
            for half in range(2):
                cols = slice(half * HALF, (half + 1) * HALF)
                nc.scalar.activation(h_bf[e][:, cols, :], banks[(e, half)][:].rearrange("p t n -> p n t"), SILU)

        def second_layer(e, c0, c1):
            nc.vector.quantize_mx(
                out=h_codes[e][:, c0:c1].bitcast(FP8X4),
                scales=h_scales[e][:, c0:c1],
                in_=h_bf[e][:, c0:c1, :].rearrange("p n t -> p (n t)"),
            )
            y_ps = psum_y.tile([P, c1 - c0], F32, name="y_ps")
            nc.tensor.matmul_mx(
                out=y_ps[:],
                lhsT=w2_codes[e][:].bitcast(FP8X4),
                lhsT_scale=w2_scales[e][:],
                rhs=h_codes[e][:, c0:c1].bitcast(FP8X4),
                rhs_scale=h_scales[e][:, c0:c1],
                start=True,
                stop=True,
            )
            return y_ps

        def scatter(e, c0, c1, y_ps):
            nc.scalar.copy(y_sb[e][:, c0:c1], y_ps[:])
            put(e, c0, c1)

        def put(e, c0, c1):
            places = dst_sb[:, (e * C + c0) // 16 : (e * C + c1) // 16]
            nc.vector.tensor_tensor(out_sb[:].indirect(places), y_sb[e][:, c0:c1], gate_sb[:, e * C + c0 : e * C + c1], MULT)

        nc.vector.memset(tok_scales[:], 0)
        build_identity()
        nc.scalar.activation(warm_out[:], ones[:, 0:16], SILU)

        load_words(0)
        nc.sync.dma_start(offs_sb[:], offs)
        nc.sync.dma_start(out=gate_col[:], in_=gate[0].rearrange("(p c) -> p c", p=P))
        load_scales(0)
        load_w1(0, 0)
        load_scales(1)
        load_w1(0, 1)
        load_words(1)
        for e in range(1, E):
            if e == E - 1:
                load_w2(e - 1)
            load_w1(e, 0)
            if e < E - 1:
                load_w2(e - 1)
            if e == 1:
                nc.sync.dma_start(dst_sb[:], dst)
            load_w1(e, 1)
        load_w2(E - 1)

        spread_gate()
        gather_scales(0)
        gather_scales(1)
        cast_w1(nc.scalar.copy, 0, 0, 0, P, 0, PACK)
        gather_words(0, 0)
        gather_words(1, 0)
        quantise_w1(0, 0, 0, PACK)
        first_layer(0, 0)
        cast_w1(nc.scalar.copy, 0, 1, 0, P, 0, PACK)
        gather_words(0, 1)
        quantise_w1(0, 1, 0, PACK)
        first_layer(0, 1)
        gather_words(1, 1)
        for e in range(1, E - 1):
            scalar_end = P - VECTOR_SHARE
            cast_w1(nc.scalar.copy, e, 0, 0, UNDER_H // 2, 0, PACK)
            cast_w1(nc.scalar.copy, e, 0, UNDER_H // 2, UNDER_H, 0, PACK)
            cast_w1(nc.scalar.copy, e, 0, UNDER_H, scalar_end, 0, 2)
            silu(e - 1)
            cast_w1(nc.scalar.copy, e, 0, UNDER_H, scalar_end, 2, PACK)
            cast_w1(nc.vector.tensor_copy, e, 0, scalar_end, P, 0, PACK)
            cast_w2(nc.vector.tensor_copy, e - 1)
            quantise_w2(e - 1)
            quantise_w1(e, 0, 0, 2)
            y_ps = second_layer(e - 1, 0, C)
            quantise_w1(e, 0, 2, PACK)
            first_layer(e, 0)

            if e == 1:
                cast_w1(nc.scalar.copy, e, 1, 0, FIRST_PART, 0, PACK)
                cast_w1(nc.scalar.copy, e, 1, FIRST_PART, scalar_end, 0, PACK)
            else:
                scalar_end = P - SH21
                cast_w1(nc.scalar.copy, e, 1, 0, scalar_end, 0, PACK)
            cast_w1(nc.vector.tensor_copy, e, 1, scalar_end, P, 0, PACK)
            quantise_w1(e, 1, 0, 2)
            quantise_w1(e, 1, 2, PACK)
            first_layer(e, 1)
            if e == 1:
                scatter(0, 0, C, y_ps)
            else:
                nc.scalar.copy(y_sb[1][:, HALF:C], y_ps[:, HALF:C])
                put(1, HALF, C)
        y_held = y_ps

        cast_w2(nc.scalar.copy, 2)
        quantise_w2(2)
        nc.vector.tensor_tensor(y_gated, y_held[:, 0:HALF], gate_sb[:, C : C + HALF], MULT)
        silu(2)
        nc.scalar.activation(out_sb[:].indirect(dst_sb[:, C // 16 : (C + HALF) // 16]), y_gated, COPY)
        cast_pair(nc.vector.tensor_copy, 1, 0, P)
        cast_pair(nc.vector.tensor_copy, 0, 0, P)
        quantise_pair(1)
        quantise_pair(0)
        y_ps = second_layer(2, 0, C)
        first_layer(3, 0)
        cast_w1(nc.scalar.copy, 3, 1, 0, P - SH31, 0, PACK)
        cast_w1(nc.vector.tensor_copy, 3, 1, P - SH31, P, 0, PACK)
        quantise_w1(3, 1, 0, 2)
        quantise_w1(3, 1, 2, 3)
        quantise_w1(3, 1, 3, PACK)
        first_layer(3, 1)
        scatter(2, 0, C, y_ps)

        cast_w2(nc.scalar.copy, E - 1)
        quantise_w2(E - 1)
        silu(E - 1)
        y_halves = [second_layer(E - 1, half * HALF, (half + 1) * HALF) for half in range(2)]
        for half in range(2):
            scatter(E - 1, half * HALF, (half + 1) * HALF, y_halves[half])
        nc.sync.dma_start(out=out, in_=out_sb[:])
